import numpy as np
import ml_dtypes


def mxq(x, axis, fmt="e4m3"):
    dtype, down = {"e4m3": (ml_dtypes.float8_e4m3fn, 7), "e5m2": (ml_dtypes.float8_e5m2, 14)}[fmt]
    v = np.moveaxis(np.asarray(x, np.float32).astype(ml_dtypes.bfloat16).astype(np.float64), axis, -1)
    blocks = v.reshape(v.shape[:-1] + (-1, 32))
    amax = np.abs(blocks).max(-1, keepdims=True)
    byte = np.maximum(np.where(amax > 0, np.frexp(amax)[1] - 1 + 127, 0) - down, 1)
    scale = np.exp2(byte - 127.0)
    codes = (blocks / scale).astype(np.float32).astype(dtype).astype(np.float64)
    return np.moveaxis((codes * scale).reshape(v.shape), -1, axis)


WIDE = False


def mx_kscale(k):
    if not WIDE:
        return np.ones(k)
    levels = np.array([10, -10, 5, -5, 0])
    if k % 512:
        return np.exp2(np.random.permutation(np.resize(levels, k // 32))).repeat(32)
    a = np.empty((k // 512, 16))
    for p in range(k // 512):
        a[p, :8] = np.random.permutation(np.resize(levels, 8))
        for g in range(8):
            far = levels[np.abs(levels - a[p, g]) >= 10]
            a[p, g + 8] = far[np.random.randint(len(far))]
    return np.exp2(a.ravel()).repeat(32)


def f64(x):
    return np.asarray(x).astype(np.float64)


def striped(idx):
    return np.tile(np.asarray(idx).reshape(-1, 16).T, (8, 1)).astype(np.uint16)


def unstriped(offs):
    return offs[:16].T.reshape(-1).astype(np.int64)


E2M1 = np.array([0.0, 0.5, 1.0, 1.5, 2.0, 3.0, 4.0, 6.0, -0.0, -0.5, -1.0, -1.5, -2.0, -3.0, -4.0, -6.0])


def pack_weight(w, fmt):
    k, n = w.shape
    w = f64(np.asarray(w, np.float32).astype(ml_dtypes.bfloat16)).reshape(k // 32, 32, n)
    amax = np.abs(w).max(1)
    if fmt == "e4m3":
        byte = np.frexp(amax)[1] - 1 + 127 - 7
    else:
        mant, ex = np.frexp(amax / 6.0)
        byte = np.where(mant > 0.5, ex, ex - 1) + 127
    byte = np.clip(np.where(amax > 0, byte, 1), 1, 254)
    scaled = (w * np.exp2(127.0 - byte)[:, None, :]).reshape(k, n).astype(np.float32)
    by_word = np.ascontiguousarray(scaled.reshape(k // 512, 128, 4, n).transpose(0, 1, 3, 2))
    if fmt == "e4m3":
        words = by_word.astype(ml_dtypes.float8_e4m3fn).view(np.uint8)
    else:
        c = by_word.astype(ml_dtypes.float4_e2m1fn).view(np.uint8) & 0xF
        words = (c[..., 0::2] | (c[..., 1::2] << 4)).reshape(k // 512, 128, 2 * n)
    return np.ascontiguousarray(words), np.ascontiguousarray(byte.astype(np.uint8).reshape(k // 512, 16, n))


def unpack_weight(words, scales, fmt):
    g, _, n = scales.shape
    words = np.ascontiguousarray(words).reshape(g, 128, n, -1)
    if fmt == "e4m3":
        vals = words.view(ml_dtypes.float8_e4m3fn).astype(np.float64)
    else:
        nib = np.empty((g, 128, n, 4), np.uint8)
        nib[..., 0::2] = words & 0xF
        nib[..., 1::2] = words >> 4
        vals = E2M1[nib]
    vals = vals * np.repeat(np.exp2(scales.astype(np.float64) - 127.0), 8, axis=1)[..., None]
    return vals.transpose(0, 1, 3, 2).reshape(g * 512, n)


def sigmoid(v):
    return 1.0 / (1.0 + np.exp(-v))


B, N, T, D, NQ = 1, 512, 2048, 512, 256


def setup_inputs():
    n = np.random.standard_normal
    idx = np.random.permutation(T)[:B * N]
    s = mx_kscale(D)[:, None]
    kp = pack_weight(n((D, T)) / s, "e4m3")
    return {
        "qT": (n((B, D, NQ)) * s * (1.00 / np.sqrt(D))).astype(np.float32),
        "k_words": kp[0],
        "k_scales": kp[1],
        "kb": np.tile(n(2048), (128, 1)).astype(np.float32),
        "offs": striped(idx),
    }


def reference(qT, k_words, k_scales, kb, offs):
    idx = unstriped(offs)
    pick = lambda x, which: x[:, which].reshape(x.shape[0], B, -1).transpose(1, 0, 2)
    k = unpack_weight(k_words, k_scales, "e4m3")
    kg = pick(k, idx)
    qq = mxq(f64(qT), 1, "e4m3")
    a = qq.transpose(0, 2, 1) @ kg
    x = sigmoid(a + pick(f64(kb), idx)[:, :1, :])
    y = x / np.sum(x, axis=-1, keepdims=True) * 2.5
    return y

@@ -1,0 +1,117 @@
+from contextlib import ExitStack
+
+import concourse.mybir as mybir
+from concourse.masks import make_identity
+
+F32 = mybir.dt.float32
+BF16 = mybir.dt.bfloat16
+I32 = mybir.dt.int32
+U32 = mybir.dt.uint32
+U16 = mybir.dt.uint16
+U8 = mybir.dt.uint8
+FP8X4 = mybir.dt.float8_e4m3fn_x4
+ALU = mybir.AluOpType
+ACT = mybir.ActivationFunctionType
+
+P = 128
+PACK = 4
+D, T, N, NQ = 512, 2048, 512, 256
+HALF = N // 2
+BIAS_ROW = P - 1
+FLOPS = 2 * NQ * N * D
+BYTES = D * NQ * 4 + P * T * 4 + 16 * T + T * 4 + P * (N // 16) * 2 + NQ * N * 4
+
+
+def tile_attend_nrm_sig_topk_kernel(tc, qT, k_words, k_scales, kb, offs, out):
+    nc = tc.nc
+    with ExitStack() as ctx:
+        sb = ctx.enter_context(tc.tile_pool(name="sb", bufs=1))
+        ps = ctx.enter_context(tc.psum_pool(name="ps", bufs=1))
+
+        offsets = sb.tile([P, N // 16], U16, name="offsets")
+        kb_pool = sb.tile([P, T], F32, name="kb_pool", align_bytes=64)
+        scale_pool = sb.tile([P, T // 4], I32, name="scale_pool", align_bytes=64)
+        word_pool = sb.tile([P, T], I32, name="word_pool", align_bytes=64)
+        q_raw = sb.tile([P, PACK, NQ], F32, name="q_raw", align_bytes=64)
+        ident = sb.tile([P, P], F32, name="ident", align_bytes=64)
+
+        nc.sync.dma_start(offsets[:], offs)
+        nc.sync.dma_start(kb_pool[BIAS_ROW:P, :], kb[0:1, :])
+        nc.vector.memset(scale_pool[:], 0)
+        nc.vector.memset(kb_pool[0:BIAS_ROW, :], 0.0)
+        nc.sync.dma_start(q_raw[:], qT[0].rearrange("(p j) w -> p j w", j=PACK))
+        scale_rows = k_scales[0].bitcast(I32)
+        for quad in range(4):
+            nc.sync.dma_start(scale_pool[32 * quad : 32 * quad + 4, :], scale_rows[4 * quad : 4 * quad + 4, :])
+        nc.sync.dma_start(word_pool[:], k_words[0].rearrange("p t r -> p (t r)").bitcast(I32))
+
+        warm = sb.tile([P, 1], F32, name="warm")
+        warm_in = sb.tile([P, 1], F32, name="warm_in")
+        nc.gpsimd.memset(warm_in[:], 0.0)
+        nc.scalar.activation(warm[:], warm_in[:], ACT.Sigmoid)
+        make_identity(nc, ident[:])
+
+        kb_listed = sb.tile([P, N], F32, name="kb_listed", align_bytes=64)
+        nc.vector.tensor_copy(kb_listed[:], kb_pool[:].indirect(offsets[:]))
+        key_scales = sb.tile([P, N], U8, name="key_scales", align_bytes=64)
+        nc.vector.tensor_copy(key_scales[:], scale_pool[:].bitcast(U8).indirect(offsets[:]))
+
+        turned = ps.tile([P, N // P, P], F32, name="turned")
+        for s in range(N // P):
+            nc.tensor.transpose(turned[:, s, :], kb_listed[:, s * P : (s + 1) * P], ident[:])
+
+        q_bf = sb.tile([P, NQ, PACK], BF16, name="q_bf", align_bytes=64)
+        bias_col = sb.tile([P, N // P], F32, name="bias_col")
+        nc.scalar.copy(
+            q_bf[:].rearrange("p (c i) t -> p c t i", i=4),
+            q_raw[:].rearrange("p t (c i) -> p c t i", i=4),
+        )
+        nc.scalar.copy(bias_col[:], turned[:, :, BIAS_ROW])
+        q_codes = sb.tile([P, NQ], U32, name="q_codes", align_bytes=64)
+        q_scales = sb.tile([P, NQ], U8, name="q_scales", align_bytes=64)
+        nc.vector.quantize_mx(q_codes[:].bitcast(FP8X4), q_scales[:], q_bf[:].rearrange("p w t -> p (w t)"))
+
+        bias = []
+        for h in range(2):
+            spread = ps.tile([P, HALF], F32, name="spread%d" % h)
+            for u in range(2):
+                s = 2 * h + u
+                nc.tensor.transpose(spread[:, u * P : (u + 1) * P], bias_col[:, s : s + 1].to_broadcast([P, P]), ident[:])
+            bias_h = sb.tile([P, HALF], F32, name="bias%d" % h, align_bytes=64)
+            nc.scalar.copy(bias_h[:], spread[:])
+            bias.append(bias_h)
+
+        scores = {}
+        for h in range(2):
+            key_words = sb.tile([P, HALF], U32, name="key_words%d" % h, align_bytes=64)
+            nc.vector.tensor_copy(key_words[:], word_pool[:].bitcast(U32).indirect(offsets[:, 16 * h : 16 * (h + 1)]))
+            for g in range(2):
+                acc = ps.tile([P, HALF], F32, name="acc%d%d" % (g, h))
+                nc.tensor.matmul_mx(
+                    acc[:],
+                    lhsT=q_codes[:, g * P : (g + 1) * P].bitcast(FP8X4),
+                    lhsT_scale=q_scales[:, g * P : (g + 1) * P],
+                    rhs=key_words[:].bitcast(FP8X4),
+                    rhs_scale=key_scales[:, h * HALF : (h + 1) * HALF],
+                    start=True,
+                    stop=True,
+                )
+                scores[g, h] = acc
+
+        gates = [sb.tile([P, N], F32, name="gates%d" % g, align_bytes=64) for g in range(2)]
+        sums = [sb.tile([P, 2], F32, name="sums%d" % g) for g in range(2)]
+        for h in range(2):
+            for g in range(2):
+                logits = sb.tile([P, HALF], F32, name="logits%d%d" % (g, h), align_bytes=64)
+                nc.vector.tensor_tensor(logits[:], scores[g, h][:], bias[h][:], ALU.add)
+                nc.scalar.activation(
+                    gates[g][:, h * HALF : (h + 1) * HALF], logits[:], ACT.Sigmoid, accum_out=sums[g][:, h : h + 1]
+                )
+        for g in range(2):
+            total = sb.tile([P, 1], F32, name="total%d" % g)
+            nc.vector.tensor_scalar(total[:], sums[g][:, 0:1], sums[g][:, 1:2], None, ALU.add)
+            inverse = sb.tile([P, 1], F32, name="inverse%d" % g)
+            nc.vector.reciprocal(inverse[:], total[:])
+            result = sb.tile([P, N], F32, name="result%d" % g, align_bytes=64)
+            nc.vector.tensor_scalar(result[:], gates[g][:], inverse[:], 2.5, ALU.mult, ALU.mult)
+            nc.sync.dma_start(out[0, g * P : (g + 1) * P, :], result[:])

@@ -18,6 +18,7 @@ PACK = 4
 D, T, N, NQ = 512, 2048, 512, 256
 HALF = N // 2
 BIAS_ROW = P - 1
+ZERO_SPLIT = 768
 FLOPS = 2 * NQ * N * D
 BYTES = D * NQ * 4 + P * T * 4 + 16 * T + T * 4 + P * (N // 16) * 2 + NQ * N * 4
 
@@ -29,16 +30,22 @@ def tile_attend_nrm_sig_topk_kernel(tc, qT, k_words, k_scales, kb, offs, out):
         ps = ctx.enter_context(tc.psum_pool(name="ps", bufs=1))
 
         offsets = sb.tile([P, N // 16], U16, name="offsets")
-        kb_pool = sb.tile([P, T], F32, name="kb_pool", align_bytes=64)
-        scale_pool = sb.tile([P, T // 4], I32, name="scale_pool", align_bytes=64)
+        kb_pool = sb.tile([P, T], F32, name="kb_pool", tag="kb", align_bytes=64)
+        scale_pool = sb.tile([P, T // 4], I32, name="scale_pool", tag="scales", align_bytes=64)
         word_pool = sb.tile([P, T], I32, name="word_pool", align_bytes=64)
-        q_raw = sb.tile([P, PACK, NQ], F32, name="q_raw", align_bytes=64)
+        q_raw = sb.tile([P, PACK, NQ], F32, name="q_raw", tag="raw", align_bytes=64)
         ident = sb.tile([P, P], F32, name="ident", align_bytes=64)
 
         nc.sync.dma_start(offsets[:], offs)
         nc.sync.dma_start(kb_pool[BIAS_ROW:P, :], kb[0:1, :])
-        nc.vector.memset(scale_pool[:], 0)
-        nc.vector.memset(kb_pool[0:BIAS_ROW, :], 0.0)
+        warm_in = sb.tile([P, 1], F32, name="warm_in")
+        nc.gpsimd.memset(warm_in[:], 0.0)
+        nc.gpsimd.memset(kb_pool[0:BIAS_ROW, ZERO_SPLIT:T], 0.0)
+        make_identity(nc, ident[:])
+        nc.vector.memset(scale_pool[:, 0 : T // 4 - 1], 0)
+        nc.vector.memset(scale_pool[:, T // 4 - 1 : T // 4], 0)
+        nc.vector.memset(kb_pool[0:BIAS_ROW, 0 : ZERO_SPLIT - 1], 0.0)
+        nc.vector.memset(kb_pool[0:BIAS_ROW, ZERO_SPLIT - 1 : ZERO_SPLIT], 0.0)
         nc.sync.dma_start(q_raw[:], qT[0].rearrange("(p j) w -> p j w", j=PACK))
         scale_rows = k_scales[0].bitcast(I32)
         for quad in range(4):
@@ -46,72 +53,75 @@ def tile_attend_nrm_sig_topk_kernel(tc, qT, k_words, k_scales, kb, offs, out):
         nc.sync.dma_start(word_pool[:], k_words[0].rearrange("p t r -> p (t r)").bitcast(I32))
 
         warm = sb.tile([P, 1], F32, name="warm")
-        warm_in = sb.tile([P, 1], F32, name="warm_in")
-        nc.gpsimd.memset(warm_in[:], 0.0)
         nc.scalar.activation(warm[:], warm_in[:], ACT.Sigmoid)
-        make_identity(nc, ident[:])
 
         kb_listed = sb.tile([P, N], F32, name="kb_listed", align_bytes=64)
         nc.vector.tensor_copy(kb_listed[:], kb_pool[:].indirect(offsets[:]))
-        key_scales = sb.tile([P, N], U8, name="key_scales", align_bytes=64)
+        key_scales = sb.tile([P, N], U8, name="key_scales", tag="kb", align_bytes=64)
         nc.vector.tensor_copy(key_scales[:], scale_pool[:].bitcast(U8).indirect(offsets[:]))
 
         turned = ps.tile([P, N // P, P], F32, name="turned")
         for s in range(N // P):
             nc.tensor.transpose(turned[:, s, :], kb_listed[:, s * P : (s + 1) * P], ident[:])
 
-        q_bf = sb.tile([P, NQ, PACK], BF16, name="q_bf", align_bytes=64)
-        bias_col = sb.tile([P, N // P], F32, name="bias_col")
+        q_bf = sb.tile([P, NQ, PACK], BF16, name="q_bf", tag="packed", align_bytes=64)
         nc.scalar.copy(
             q_bf[:].rearrange("p (c i) t -> p c t i", i=4),
             q_raw[:].rearrange("p t (c i) -> p c t i", i=4),
         )
+        bias_col = sb.tile([P, N // P], F32, name="bias_col", tag="raw", align_bytes=64)
         nc.scalar.copy(bias_col[:], turned[:, :, BIAS_ROW])
         q_codes = sb.tile([P, NQ], U32, name="q_codes", align_bytes=64)
-        q_scales = sb.tile([P, NQ], U8, name="q_scales", align_bytes=64)
+        q_scales = sb.tile([P, NQ], U8, name="q_scales", tag="scales", align_bytes=64)
         nc.vector.quantize_mx(q_codes[:].bitcast(FP8X4), q_scales[:], q_bf[:].rearrange("p w t -> p (w t)"))
 
-        bias = []
+        bias = sb.tile([P, N], F32, name="bias", align_bytes=64)
         for h in range(2):
             spread = ps.tile([P, HALF], F32, name="spread%d" % h)
             for u in range(2):
                 s = 2 * h + u
                 nc.tensor.transpose(spread[:, u * P : (u + 1) * P], bias_col[:, s : s + 1].to_broadcast([P, P]), ident[:])
-            bias_h = sb.tile([P, HALF], F32, name="bias%d" % h, align_bytes=64)
-            nc.scalar.copy(bias_h[:], spread[:])
-            bias.append(bias_h)
+            nc.scalar.copy(bias[:, h * HALF : (h + 1) * HALF], spread[:])
 
         scores = {}
+        key_words = sb.tile([P, N], U32, name="key_words", tag="packed", align_bytes=64)
         for h in range(2):
-            key_words = sb.tile([P, HALF], U32, name="key_words%d" % h, align_bytes=64)
-            nc.vector.tensor_copy(key_words[:], word_pool[:].bitcast(U32).indirect(offsets[:, 16 * h : 16 * (h + 1)]))
+            slots = slice(h * HALF, (h + 1) * HALF)
+            nc.vector.tensor_copy(key_words[:, slots], word_pool[:].bitcast(U32).indirect(offsets[:, 16 * h : 16 * (h + 1)]))
             for g in range(2):
-                acc = ps.tile([P, HALF], F32, name="acc%d%d" % (g, h))
+                scores[g, h] = ps.tile([P, HALF], F32, name="scores%d%d" % (g, h))
                 nc.tensor.matmul_mx(
-                    acc[:],
+                    scores[g, h][:],
                     lhsT=q_codes[:, g * P : (g + 1) * P].bitcast(FP8X4),
                     lhsT_scale=q_scales[:, g * P : (g + 1) * P],
-                    rhs=key_words[:].bitcast(FP8X4),
-                    rhs_scale=key_scales[:, h * HALF : (h + 1) * HALF],
+                    rhs=key_words[:, slots].bitcast(FP8X4),
+                    rhs_scale=key_scales[:, slots],
                     start=True,
                     stop=True,
                 )
-                scores[g, h] = acc
 
         gates = [sb.tile([P, N], F32, name="gates%d" % g, align_bytes=64) for g in range(2)]
         sums = [sb.tile([P, 2], F32, name="sums%d" % g) for g in range(2)]
         for h in range(2):
+            slots = slice(h * HALF, (h + 1) * HALF)
             for g in range(2):
                 logits = sb.tile([P, HALF], F32, name="logits%d%d" % (g, h), align_bytes=64)
-                nc.vector.tensor_tensor(logits[:], scores[g, h][:], bias[h][:], ALU.add)
-                nc.scalar.activation(
-                    gates[g][:, h * HALF : (h + 1) * HALF], logits[:], ACT.Sigmoid, accum_out=sums[g][:, h : h + 1]
-                )
-        for g in range(2):
-            total = sb.tile([P, 1], F32, name="total%d" % g)
-            nc.vector.tensor_scalar(total[:], sums[g][:, 0:1], sums[g][:, 1:2], None, ALU.add)
-            inverse = sb.tile([P, 1], F32, name="inverse%d" % g)
-            nc.vector.reciprocal(inverse[:], total[:])
-            result = sb.tile([P, N], F32, name="result%d" % g, align_bytes=64)
-            nc.vector.tensor_scalar(result[:], gates[g][:], inverse[:], 2.5, ALU.mult, ALU.mult)
-            nc.sync.dma_start(out[0, g * P : (g + 1) * P, :], result[:])
+                nc.vector.tensor_tensor(logits[:], scores[g, h][:], bias[:, slots], ALU.add)
+                nc.scalar.activation(gates[g][:, slots], logits[:], ACT.Sigmoid, accum_out=sums[g][:, h : h + 1])
+        total = [sb.tile([P, 1], F32, name="total%d" % g) for g in range(2)]
+        inverse = [sb.tile([P, 1], F32, name="inverse%d" % g) for g in range(2)]
+        result = [sb.tile([P, N], F32, name="result%d" % g, align_bytes=64) for g in range(2)]
+
+        def add_halves(g):
+            nc.vector.tensor_scalar(total[g][:], sums[g][:, 0:1], sums[g][:, 1:2], None, ALU.add)
+
+        def normalise(g):
+            nc.vector.tensor_scalar(result[g][:], gates[g][:], inverse[g][:], 2.5, ALU.mult, ALU.mult)
+            nc.sync.dma_start(out[0, g * P : (g + 1) * P, :], result[g][:])
+
+        add_halves(0)
+        nc.vector.reciprocal(inverse[0][:], total[0][:])
+        add_halves(1)
+        normalise(0)
+        nc.vector.reciprocal(inverse[1][:], total[1][:])
+        normalise(1)

@@ -19,6 +19,8 @@ D, T, N, NQ = 512, 2048, 512, 256
 HALF = N // 2
 BIAS_ROW = P - 1
 ZERO_SPLIT = 768
+WARM_BEFORE, WARM_BETWEEN, WARM_AFTER = 10, 6, 6
+SCALE_SPLIT = 344
 FLOPS = 2 * NQ * N * D
 BYTES = D * NQ * 4 + P * T * 4 + 16 * T + T * 4 + P * (N // 16) * 2 + NQ * N * 4
 
@@ -30,10 +32,10 @@ def tile_attend_nrm_sig_topk_kernel(tc, qT, k_words, k_scales, kb, offs, out):
         ps = ctx.enter_context(tc.psum_pool(name="ps", bufs=1))
 
         offsets = sb.tile([P, N // 16], U16, name="offsets")
-        kb_pool = sb.tile([P, T], F32, name="kb_pool", tag="kb", align_bytes=64)
+        kb_pool = sb.tile([P, T], F32, name="kb_pool", align_bytes=64)
         scale_pool = sb.tile([P, T // 4], I32, name="scale_pool", tag="scales", align_bytes=64)
         word_pool = sb.tile([P, T], I32, name="word_pool", align_bytes=64)
-        q_raw = sb.tile([P, PACK, NQ], F32, name="q_raw", tag="raw", align_bytes=64)
+        q_raw = sb.tile([P, PACK, NQ], F32, name="q_raw", align_bytes=64)
         ident = sb.tile([P, P], F32, name="ident", align_bytes=64)
 
         nc.sync.dma_start(offsets[:], offs)
@@ -52,24 +54,30 @@ def tile_attend_nrm_sig_topk_kernel(tc, qT, k_words, k_scales, kb, offs, out):
             nc.sync.dma_start(scale_pool[32 * quad : 32 * quad + 4, :], scale_rows[4 * quad : 4 * quad + 4, :])
         nc.sync.dma_start(word_pool[:], k_words[0].rearrange("p t r -> p (t r)").bitcast(I32))
 
+
         warm = sb.tile([P, 1], F32, name="warm")
         nc.scalar.activation(warm[:], warm_in[:], ACT.Sigmoid)
+        spare = ps.tile([P, N // P, P], F32, name="spare")
+        for s in range(WARM_BEFORE):
+            nc.tensor.transpose(spare[:, s % 4, :], ident[:], ident[:])
 
         kb_listed = sb.tile([P, N], F32, name="kb_listed", align_bytes=64)
         nc.vector.tensor_copy(kb_listed[:], kb_pool[:].indirect(offsets[:]))
-        key_scales = sb.tile([P, N], U8, name="key_scales", tag="kb", align_bytes=64)
+        key_scales = sb.tile([P, N], U8, name="key_scales", align_bytes=64)
         nc.vector.tensor_copy(key_scales[:], scale_pool[:].bitcast(U8).indirect(offsets[:]))
 
         turned = ps.tile([P, N // P, P], F32, name="turned")
         for s in range(N // P):
             nc.tensor.transpose(turned[:, s, :], kb_listed[:, s * P : (s + 1) * P], ident[:])
+        for s in range(WARM_BETWEEN):
+            nc.tensor.transpose(spare[:, s % 4, :], kb_listed[:, 0:P], ident[:])
 
-        q_bf = sb.tile([P, NQ, PACK], BF16, name="q_bf", tag="packed", align_bytes=64)
+        q_bf = sb.tile([P, NQ, PACK], BF16, name="q_bf", align_bytes=64)
         nc.scalar.copy(
             q_bf[:].rearrange("p (c i) t -> p c t i", i=4),
             q_raw[:].rearrange("p t (c i) -> p c t i", i=4),
         )
-        bias_col = sb.tile([P, N // P], F32, name="bias_col", tag="raw", align_bytes=64)
+        bias_col = sb.tile([P, N // P], F32, name="bias_col", align_bytes=64)
         nc.scalar.copy(bias_col[:], turned[:, :, BIAS_ROW])
         q_codes = sb.tile([P, NQ], U32, name="q_codes", align_bytes=64)
         q_scales = sb.tile([P, NQ], U8, name="q_scales", tag="scales", align_bytes=64)
@@ -83,8 +91,11 @@ def tile_attend_nrm_sig_topk_kernel(tc, qT, k_words, k_scales, kb, offs, out):
                 nc.tensor.transpose(spread[:, u * P : (u + 1) * P], bias_col[:, s : s + 1].to_broadcast([P, P]), ident[:])
             nc.scalar.copy(bias[:, h * HALF : (h + 1) * HALF], spread[:])
 
+        for s in range(WARM_AFTER):
+            nc.tensor.transpose(spare[:, s % 4, :], bias_col[:, 0:1].to_broadcast([P, P]), ident[:])
+
         scores = {}
-        key_words = sb.tile([P, N], U32, name="key_words", tag="packed", align_bytes=64)
+        key_words = sb.tile([P, N], U32, name="key_words", align_bytes=64)
         for h in range(2):
             slots = slice(h * HALF, (h + 1) * HALF)
             nc.vector.tensor_copy(key_words[:, slots], word_pool[:].bitcast(U32).indirect(offsets[:, 16 * h : 16 * (h + 1)]))
@@ -100,28 +111,24 @@ def tile_attend_nrm_sig_topk_kernel(tc, qT, k_words, k_scales, kb, offs, out):
                     stop=True,
                 )
 
+        logits = [sb.tile([P, N], F32, name="logits%d" % g, align_bytes=64) for g in range(2)]
         gates = [sb.tile([P, N], F32, name="gates%d" % g, align_bytes=64) for g in range(2)]
-        sums = [sb.tile([P, 2], F32, name="sums%d" % g) for g in range(2)]
-        for h in range(2):
-            slots = slice(h * HALF, (h + 1) * HALF)
-            for g in range(2):
-                logits = sb.tile([P, HALF], F32, name="logits%d%d" % (g, h), align_bytes=64)
-                nc.vector.tensor_tensor(logits[:], scores[g, h][:], bias[:, slots], ALU.add)
-                nc.scalar.activation(gates[g][:, slots], logits[:], ACT.Sigmoid, accum_out=sums[g][:, h : h + 1])
+        half_sums = sb.tile([P, 2], F32, name="half_sums")
         total = [sb.tile([P, 1], F32, name="total%d" % g) for g in range(2)]
         inverse = [sb.tile([P, 1], F32, name="inverse%d" % g) for g in range(2)]
         result = [sb.tile([P, N], F32, name="result%d" % g, align_bytes=64) for g in range(2)]
+        for h in range(2):
+            slots = slice(h * HALF, (h + 1) * HALF)
+            for g in range(2):
+                nc.vector.tensor_tensor(logits[g][:, slots], scores[g, h][:], bias[:, slots], ALU.add)
+            nc.scalar.activation(gates[0][:, slots], logits[0][:, slots], ACT.Sigmoid, accum_out=half_sums[:, h : h + 1])
+        nc.scalar.activation(gates[1][:], logits[1][:], ACT.Sigmoid, accum_out=total[1][:])
 
-        def add_halves(g):
-            nc.vector.tensor_scalar(total[g][:], sums[g][:, 0:1], sums[g][:, 1:2], None, ALU.add)
-
-        def normalise(g):
-            nc.vector.tensor_scalar(result[g][:], gates[g][:], inverse[g][:], 2.5, ALU.mult, ALU.mult)
-            nc.sync.dma_start(out[0, g * P : (g + 1) * P, :], result[g][:])
-
-        add_halves(0)
+        nc.vector.tensor_scalar(total[0][:], half_sums[:, 0:1], half_sums[:, 1:2], 0.4, ALU.add, ALU.mult)
         nc.vector.reciprocal(inverse[0][:], total[0][:])
-        add_halves(1)
-        normalise(0)
+        nc.vector.tensor_scalar(result[0][:, :SCALE_SPLIT], gates[0][:, :SCALE_SPLIT], inverse[0][:], None, ALU.mult)
+        nc.scalar.activation(result[0][:, SCALE_SPLIT:], gates[0][:, SCALE_SPLIT:], ACT.Copy, scale=inverse[0][:])
+        nc.sync.dma_start(out[0, 0:P, :], result[0][:])
         nc.vector.reciprocal(inverse[1][:], total[1][:])
-        normalise(1)
+        nc.vector.tensor_scalar(result[1][:], gates[1][:], inverse[1][:], 2.5, ALU.mult, ALU.mult)
+        nc.sync.dma_start(out[0, P : 2 * P, :], result[1][:])

@@ -18,11 +18,11 @@ PACK = 4
 D, T, N, NQ = 512, 2048, 512, 256
 HALF = N // 2
 BIAS_ROW = P - 1
-ZERO_SPLIT = 768
-WARM_BEFORE, WARM_BETWEEN, WARM_AFTER = 10, 6, 6
-SCALE_SPLIT = 344
 FLOPS = 2 * NQ * N * D
 BYTES = D * NQ * 4 + P * T * 4 + 16 * T + T * 4 + P * (N // 16) * 2 + NQ * N * 4
+SCALE_ROW0 = 48
+ZERO_SPLIT = 1000
+SCALE_SPLIT = 344
 
 
 def tile_attend_nrm_sig_topk_kernel(tc, qT, k_words, k_scales, kb, offs, out):
@@ -33,66 +33,65 @@ def tile_attend_nrm_sig_topk_kernel(tc, qT, k_words, k_scales, kb, offs, out):
 
         offsets = sb.tile([P, N // 16], U16, name="offsets")
         kb_pool = sb.tile([P, T], F32, name="kb_pool", align_bytes=64)
-        scale_pool = sb.tile([P, T // 4], I32, name="scale_pool", tag="scales", align_bytes=64)
+        scale_pool = sb.tile([P, T // 4], I32, name="scale_pool", align_bytes=64)
         word_pool = sb.tile([P, T], I32, name="word_pool", align_bytes=64)
-        q_raw = sb.tile([P, PACK, NQ], F32, name="q_raw", align_bytes=64)
+        q_raw = sb.tile([P, PACK, NQ], F32, name="q_raw", tag="q_raw", align_bytes=64)
         ident = sb.tile([P, P], F32, name="ident", align_bytes=64)
+        key_scales = sb.tile([P, N // 4], I32, name="key_scales", align_bytes=64)
 
         nc.sync.dma_start(offsets[:], offs)
+        nc.sync.dma_start(scale_pool[SCALE_ROW0 : SCALE_ROW0 + 16, :], k_scales[0].bitcast(I32))
         nc.sync.dma_start(kb_pool[BIAS_ROW:P, :], kb[0:1, :])
-        warm_in = sb.tile([P, 1], F32, name="warm_in")
-        nc.gpsimd.memset(warm_in[:], 0.0)
-        nc.gpsimd.memset(kb_pool[0:BIAS_ROW, ZERO_SPLIT:T], 0.0)
-        make_identity(nc, ident[:])
-        nc.vector.memset(scale_pool[:, 0 : T // 4 - 1], 0)
-        nc.vector.memset(scale_pool[:, T // 4 - 1 : T // 4], 0)
-        nc.vector.memset(kb_pool[0:BIAS_ROW, 0 : ZERO_SPLIT - 1], 0.0)
-        nc.vector.memset(kb_pool[0:BIAS_ROW, ZERO_SPLIT - 1 : ZERO_SPLIT], 0.0)
         nc.sync.dma_start(q_raw[:], qT[0].rearrange("(p j) w -> p j w", j=PACK))
-        scale_rows = k_scales[0].bitcast(I32)
-        for quad in range(4):
-            nc.sync.dma_start(scale_pool[32 * quad : 32 * quad + 4, :], scale_rows[4 * quad : 4 * quad + 4, :])
         nc.sync.dma_start(word_pool[:], k_words[0].rearrange("p t r -> p (t r)").bitcast(I32))
 
+        warm_in = sb.tile([P, 1], F32, name="warm_in")
+        nc.gpsimd.memset(warm_in[:], 0.0)
+        nc.gpsimd.memset(scale_pool[64:P, :], 0)
+        nc.gpsimd.memset(kb_pool[0:BIAS_ROW, ZERO_SPLIT:T], 0.0)
+        nc.gpsimd.memset(key_scales[:], 0)
+        make_identity(nc, ident[:])
+        nc.vector.memset(scale_pool[0:SCALE_ROW0, 0 : T // 4 - 1], 0)
+        nc.vector.memset(scale_pool[0:SCALE_ROW0, T // 4 - 1 : T // 4], 0)
+        nc.vector.memset(kb_pool[0:BIAS_ROW, 0 : ZERO_SPLIT - 1], 0.0)
+        nc.vector.memset(kb_pool[0:BIAS_ROW, ZERO_SPLIT - 1 : ZERO_SPLIT], 0.0)
 
         warm = sb.tile([P, 1], F32, name="warm")
         nc.scalar.activation(warm[:], warm_in[:], ACT.Sigmoid)
-        spare = ps.tile([P, N // P, P], F32, name="spare")
-        for s in range(WARM_BEFORE):
-            nc.tensor.transpose(spare[:, s % 4, :], ident[:], ident[:])
 
-        kb_listed = sb.tile([P, N], F32, name="kb_listed", align_bytes=64)
-        nc.vector.tensor_copy(kb_listed[:], kb_pool[:].indirect(offsets[:]))
-        key_scales = sb.tile([P, N], U8, name="key_scales", align_bytes=64)
-        nc.vector.tensor_copy(key_scales[:], scale_pool[:].bitcast(U8).indirect(offsets[:]))
-
-        turned = ps.tile([P, N // P, P], F32, name="turned")
-        for s in range(N // P):
-            nc.tensor.transpose(turned[:, s, :], kb_listed[:, s * P : (s + 1) * P], ident[:])
-        for s in range(WARM_BETWEEN):
-            nc.tensor.transpose(spare[:, s % 4, :], kb_listed[:, 0:P], ident[:])
+        listed_scales = sb.tile([P, N], U8, name="listed_scales", align_bytes=64)
+        nc.vector.tensor_copy(listed_scales[:], scale_pool[:].bitcast(U8).indirect(offsets[:]))
+        for quad in range(4):
+            rows = slice(SCALE_ROW0 + 4 * quad, SCALE_ROW0 + 4 * quad + 4)
+            nc.sync.dma_start(key_scales[32 * quad : 32 * quad + 4, :], listed_scales[rows, :].bitcast(I32))
 
         q_bf = sb.tile([P, NQ, PACK], BF16, name="q_bf", align_bytes=64)
         nc.scalar.copy(
             q_bf[:].rearrange("p (c i) t -> p c t i", i=4),
             q_raw[:].rearrange("p t (c i) -> p c t i", i=4),
         )
-        bias_col = sb.tile([P, N // P], F32, name="bias_col", align_bytes=64)
-        nc.scalar.copy(bias_col[:], turned[:, :, BIAS_ROW])
+
+        kb_listed = sb.tile([P, N], F32, name="kb_listed", align_bytes=64)
+        bias_col = sb.tile([P, N // P], F32, name="bias_col", tag="q_raw", align_bytes=64)
+        bias = sb.tile([P, N], F32, name="bias", align_bytes=64)
+        for h in range(2):
+            slots = slice(h * HALF, (h + 1) * HALF)
+            nc.vector.tensor_copy(kb_listed[:, slots], kb_pool[:].indirect(offsets[:, 16 * h : 16 * (h + 1)]))
+            turned = ps.tile([P, 2, P], F32, name="turned%d" % h)
+            for u in range(2):
+                s = 2 * h + u
+                nc.tensor.transpose(turned[:, u, :], kb_listed[:, s * P : (s + 1) * P], ident[:])
+            nc.scalar.copy(bias_col[:, 2 * h : 2 * h + 2], turned[:, :, BIAS_ROW])
         q_codes = sb.tile([P, NQ], U32, name="q_codes", align_bytes=64)
-        q_scales = sb.tile([P, NQ], U8, name="q_scales", tag="scales", align_bytes=64)
+        q_scales = sb.tile([P, NQ], U8, name="q_scales", align_bytes=64)
         nc.vector.quantize_mx(q_codes[:].bitcast(FP8X4), q_scales[:], q_bf[:].rearrange("p w t -> p (w t)"))
 
-        bias = sb.tile([P, N], F32, name="bias", align_bytes=64)
         for h in range(2):
             spread = ps.tile([P, HALF], F32, name="spread%d" % h)
             for u in range(2):
                 s = 2 * h + u
                 nc.tensor.transpose(spread[:, u * P : (u + 1) * P], bias_col[:, s : s + 1].to_broadcast([P, P]), ident[:])
             nc.scalar.copy(bias[:, h * HALF : (h + 1) * HALF], spread[:])
-
-        for s in range(WARM_AFTER):
-            nc.tensor.transpose(spare[:, s % 4, :], bias_col[:, 0:1].to_broadcast([P, P]), ident[:])
 
         scores = {}
         key_words = sb.tile([P, N], U32, name="key_words", align_bytes=64)
@@ -106,7 +105,7 @@ def tile_attend_nrm_sig_topk_kernel(tc, qT, k_words, k_scales, kb, offs, out):
                     lhsT=q_codes[:, g * P : (g + 1) * P].bitcast(FP8X4),
                     lhsT_scale=q_scales[:, g * P : (g + 1) * P],
                     rhs=key_words[:, slots].bitcast(FP8X4),
-                    rhs_scale=key_scales[:, slots],
+                    rhs_scale=key_scales[:].bitcast(U8)[:, slots],
                     start=True,
                     stop=True,
                 )

@@ -23,6 +23,7 @@ BYTES = D * NQ * 4 + P * T * 4 + 16 * T + T * 4 + P * (N // 16) * 2 + NQ * N * 4
 SCALE_ROW0 = 48
 ZERO_SPLIT = 1000
 SCALE_SPLIT = 344
+BANK_OF = {(0, 0): "turned1", (1, 0): "spread0", (0, 1): "spread2", (1, 1): "spread3"}
 
 
 def tile_attend_nrm_sig_topk_kernel(tc, qT, k_words, k_scales, kb, offs, out):
@@ -40,8 +41,8 @@ def tile_attend_nrm_sig_topk_kernel(tc, qT, k_words, k_scales, kb, offs, out):
         key_scales = sb.tile([P, N // 4], I32, name="key_scales", align_bytes=64)
 
         nc.sync.dma_start(offsets[:], offs)
-        nc.sync.dma_start(scale_pool[SCALE_ROW0 : SCALE_ROW0 + 16, :], k_scales[0].bitcast(I32))
-        nc.sync.dma_start(kb_pool[BIAS_ROW:P, :], kb[0:1, :])
+        nc.scalar.dma_start(scale_pool[SCALE_ROW0 : SCALE_ROW0 + 16, :], k_scales[0].bitcast(I32))
+        nc.scalar.dma_start(kb_pool[BIAS_ROW:P, :], kb[0:1, :])
         nc.sync.dma_start(q_raw[:], qT[0].rearrange("(p j) w -> p j w", j=PACK))
         nc.sync.dma_start(word_pool[:], k_words[0].rearrange("p t r -> p (t r)").bitcast(I32))
 
@@ -77,7 +78,7 @@ def tile_attend_nrm_sig_topk_kernel(tc, qT, k_words, k_scales, kb, offs, out):
         for h in range(2):
             slots = slice(h * HALF, (h + 1) * HALF)
             nc.vector.tensor_copy(kb_listed[:, slots], kb_pool[:].indirect(offsets[:, 16 * h : 16 * (h + 1)]))
-            turned = ps.tile([P, 2, P], F32, name="turned%d" % h)
+            turned = ps.tile([P, 2, P], F32, name="turned%d" % h, tag="turned%d" % h)
             for u in range(2):
                 s = 2 * h + u
                 nc.tensor.transpose(turned[:, u, :], kb_listed[:, s * P : (s + 1) * P], ident[:])
@@ -86,12 +87,12 @@ def tile_attend_nrm_sig_topk_kernel(tc, qT, k_words, k_scales, kb, offs, out):
         q_scales = sb.tile([P, NQ], U8, name="q_scales", align_bytes=64)
         nc.vector.quantize_mx(q_codes[:].bitcast(FP8X4), q_scales[:], q_bf[:].rearrange("p w t -> p (w t)"))
 
-        for h in range(2):
-            spread = ps.tile([P, HALF], F32, name="spread%d" % h)
-            for u in range(2):
-                s = 2 * h + u
+        for first, count in ((0, 2), (2, 1), (3, 1)):
+            spread = ps.tile([P, count * P], F32, name="spread%d" % first, tag="spread%d" % first)
+            for u in range(count):
+                s = first + u
                 nc.tensor.transpose(spread[:, u * P : (u + 1) * P], bias_col[:, s : s + 1].to_broadcast([P, P]), ident[:])
-            nc.scalar.copy(bias[:, h * HALF : (h + 1) * HALF], spread[:])
+            nc.scalar.copy(bias[:, first * P : (first + count) * P], spread[:])
 
         scores = {}
         key_words = sb.tile([P, N], U32, name="key_words", align_bytes=64)
@@ -99,7 +100,7 @@ def tile_attend_nrm_sig_topk_kernel(tc, qT, k_words, k_scales, kb, offs, out):
             slots = slice(h * HALF, (h + 1) * HALF)
             nc.vector.tensor_copy(key_words[:, slots], word_pool[:].bitcast(U32).indirect(offsets[:, 16 * h : 16 * (h + 1)]))
             for g in range(2):
-                scores[g, h] = ps.tile([P, HALF], F32, name="scores%d%d" % (g, h))
+                scores[g, h] = ps.tile([P, HALF], F32, name="scores%d%d" % (g, h), tag=BANK_OF[g, h])
                 nc.tensor.matmul_mx(
                     scores[g, h][:],
                     lhsT=q_codes[:, g * P : (g + 1) * P].bitcast(FP8X4),

@@ -17,12 +17,17 @@ P = 128
 PACK = 4
 D, T, N, NQ = 512, 2048, 512, 256
 HALF = N // 2
-BIAS_ROW = P - 1
+LIST_COLS = HALF // 16
+BLOCKS = D // 32
+GAIN = 2.5
 FLOPS = 2 * NQ * N * D
-BYTES = D * NQ * 4 + P * T * 4 + 16 * T + T * 4 + P * (N // 16) * 2 + NQ * N * 4
-SCALE_ROW0 = 48
+BYTES = D * NQ * 4 + P * T * 4 + BLOCKS * T + T * 4 + P * (N // 16) * 2 + NQ * N * 4
+
+BIAS_ROW = P - 1
+SCALE_ROW0 = 64 - BLOCKS
 ZERO_SPLIT = 1000
 SCALE_SPLIT = 344
+SPREAD_RUNS = ((0, 2), (2, 1), (3, 1))
 BANK_OF = {(0, 0): "turned1", (1, 0): "spread0", (0, 1): "spread2", (1, 1): "spread3"}
 
 
@@ -41,14 +46,12 @@ def tile_attend_nrm_sig_topk_kernel(tc, qT, k_words, k_scales, kb, offs, out):
         key_scales = sb.tile([P, N // 4], I32, name="key_scales", align_bytes=64)
 
         nc.sync.dma_start(offsets[:], offs)
-        nc.scalar.dma_start(scale_pool[SCALE_ROW0 : SCALE_ROW0 + 16, :], k_scales[0].bitcast(I32))
+        nc.scalar.dma_start(scale_pool[SCALE_ROW0 : SCALE_ROW0 + BLOCKS, :], k_scales[0].bitcast(I32))
         nc.scalar.dma_start(kb_pool[BIAS_ROW:P, :], kb[0:1, :])
         nc.sync.dma_start(q_raw[:], qT[0].rearrange("(p j) w -> p j w", j=PACK))
         nc.sync.dma_start(word_pool[:], k_words[0].rearrange("p t r -> p (t r)").bitcast(I32))
 
-        warm_in = sb.tile([P, 1], F32, name="warm_in")
-        nc.gpsimd.memset(warm_in[:], 0.0)
-        nc.gpsimd.memset(scale_pool[64:P, :], 0)
+        nc.gpsimd.memset(scale_pool[SCALE_ROW0 + BLOCKS : P, :], 0)
         nc.gpsimd.memset(kb_pool[0:BIAS_ROW, ZERO_SPLIT:T], 0.0)
         nc.gpsimd.memset(key_scales[:], 0)
         make_identity(nc, ident[:])
@@ -57,8 +60,8 @@ def tile_attend_nrm_sig_topk_kernel(tc, qT, k_words, k_scales, kb, offs, out):
         nc.vector.memset(kb_pool[0:BIAS_ROW, 0 : ZERO_SPLIT - 1], 0.0)
         nc.vector.memset(kb_pool[0:BIAS_ROW, ZERO_SPLIT - 1 : ZERO_SPLIT], 0.0)
 
-        warm = sb.tile([P, 1], F32, name="warm")
-        nc.scalar.activation(warm[:], warm_in[:], ACT.Sigmoid)
+        unread = sb.tile([P, 1], F32, name="unread")
+        nc.scalar.activation(unread[0:BIAS_ROW, :], kb_pool[0:BIAS_ROW, 0:1], ACT.Sigmoid)
 
         listed_scales = sb.tile([P, N], U8, name="listed_scales", align_bytes=64)
         nc.vector.tensor_copy(listed_scales[:], scale_pool[:].bitcast(U8).indirect(offsets[:]))
@@ -77,7 +80,8 @@ def tile_attend_nrm_sig_topk_kernel(tc, qT, k_words, k_scales, kb, offs, out):
         bias = sb.tile([P, N], F32, name="bias", align_bytes=64)
         for h in range(2):
             slots = slice(h * HALF, (h + 1) * HALF)
-            nc.vector.tensor_copy(kb_listed[:, slots], kb_pool[:].indirect(offsets[:, 16 * h : 16 * (h + 1)]))
+            half_list = offsets[:, LIST_COLS * h : LIST_COLS * (h + 1)]
+            nc.vector.tensor_copy(kb_listed[:, slots], kb_pool[:].indirect(half_list))
             turned = ps.tile([P, 2, P], F32, name="turned%d" % h, tag="turned%d" % h)
             for u in range(2):
                 s = 2 * h + u
@@ -87,18 +91,20 @@ def tile_attend_nrm_sig_topk_kernel(tc, qT, k_words, k_scales, kb, offs, out):
         q_scales = sb.tile([P, NQ], U8, name="q_scales", align_bytes=64)
         nc.vector.quantize_mx(q_codes[:].bitcast(FP8X4), q_scales[:], q_bf[:].rearrange("p w t -> p (w t)"))
 
-        for first, count in ((0, 2), (2, 1), (3, 1)):
+        for first, count in SPREAD_RUNS:
             spread = ps.tile([P, count * P], F32, name="spread%d" % first, tag="spread%d" % first)
             for u in range(count):
                 s = first + u
-                nc.tensor.transpose(spread[:, u * P : (u + 1) * P], bias_col[:, s : s + 1].to_broadcast([P, P]), ident[:])
+                column = bias_col[:, s : s + 1].to_broadcast([P, P])
+                nc.tensor.transpose(spread[:, u * P : (u + 1) * P], column, ident[:])
             nc.scalar.copy(bias[:, first * P : (first + count) * P], spread[:])
 
         scores = {}
         key_words = sb.tile([P, N], U32, name="key_words", align_bytes=64)
         for h in range(2):
             slots = slice(h * HALF, (h + 1) * HALF)
-            nc.vector.tensor_copy(key_words[:, slots], word_pool[:].bitcast(U32).indirect(offsets[:, 16 * h : 16 * (h + 1)]))
+            half_list = offsets[:, LIST_COLS * h : LIST_COLS * (h + 1)]
+            nc.vector.tensor_copy(key_words[:, slots], word_pool[:].bitcast(U32).indirect(half_list))
             for g in range(2):
                 scores[g, h] = ps.tile([P, HALF], F32, name="scores%d%d" % (g, h), tag=BANK_OF[g, h])
                 nc.tensor.matmul_mx(
@@ -124,11 +130,11 @@ def tile_attend_nrm_sig_topk_kernel(tc, qT, k_words, k_scales, kb, offs, out):
             nc.scalar.activation(gates[0][:, slots], logits[0][:, slots], ACT.Sigmoid, accum_out=half_sums[:, h : h + 1])
         nc.scalar.activation(gates[1][:], logits[1][:], ACT.Sigmoid, accum_out=total[1][:])
 
-        nc.vector.tensor_scalar(total[0][:], half_sums[:, 0:1], half_sums[:, 1:2], 0.4, ALU.add, ALU.mult)
+        nc.vector.tensor_scalar(total[0][:], half_sums[:, 0:1], half_sums[:, 1:2], 1.0 / GAIN, ALU.add, ALU.mult)
         nc.vector.reciprocal(inverse[0][:], total[0][:])
         nc.vector.tensor_scalar(result[0][:, :SCALE_SPLIT], gates[0][:, :SCALE_SPLIT], inverse[0][:], None, ALU.mult)
         nc.scalar.activation(result[0][:, SCALE_SPLIT:], gates[0][:, SCALE_SPLIT:], ACT.Copy, scale=inverse[0][:])
         nc.sync.dma_start(out[0, 0:P, :], result[0][:])
         nc.vector.reciprocal(inverse[1][:], total[1][:])
-        nc.vector.tensor_scalar(result[1][:], gates[1][:], inverse[1][:], 2.5, ALU.mult, ALU.mult)
+        nc.vector.tensor_scalar(result[1][:], gates[1][:], inverse[1][:], GAIN, ALU.mult, ALU.mult)
         nc.sync.dma_start(out[0, P : 2 * P, :], result[1][:])

@@ -26,9 +26,15 @@ BYTES = D * NQ * 4 + P * T * 4 + BLOCKS * T + T * 4 + P * (N // 16) * 2 + NQ * N
 BIAS_ROW = P - 1
 SCALE_ROW0 = 64 - BLOCKS
 ZERO_SPLIT = 1000
-SCALE_SPLIT = 344
-SPREAD_RUNS = ((0, 2), (2, 1), (3, 1))
-BANK_OF = {(0, 0): "turned1", (1, 0): "spread0", (0, 1): "spread2", (1, 1): "spread3"}
+SPREAD_RUNS = ((0, 1), (1, 1), (2, 1), (3, 1))
+PIECES = (
+    (0, 0, 256, "turned1"),
+    (1, 0, 256, "spread0"),
+    (0, 256, 128, "spread1"),
+    (0, 384, 128, "spread2"),
+    (1, 256, 256, "spread3"),
+)
+ADD_ORDER = (0, 2, 3, 1, 4)
 
 
 def tile_attend_nrm_sig_topk_kernel(tc, qT, k_words, k_scales, kb, offs, out):
@@ -99,42 +105,39 @@ def tile_attend_nrm_sig_topk_kernel(tc, qT, k_words, k_scales, kb, offs, out):
                 nc.tensor.transpose(spread[:, u * P : (u + 1) * P], column, ident[:])
             nc.scalar.copy(bias[:, first * P : (first + count) * P], spread[:])
 
-        scores = {}
         key_words = sb.tile([P, N], U32, name="key_words", align_bytes=64)
+        scores = []
         for h in range(2):
             slots = slice(h * HALF, (h + 1) * HALF)
             half_list = offsets[:, LIST_COLS * h : LIST_COLS * (h + 1)]
             nc.vector.tensor_copy(key_words[:, slots], word_pool[:].bitcast(U32).indirect(half_list))
-            for g in range(2):
-                scores[g, h] = ps.tile([P, HALF], F32, name="scores%d%d" % (g, h), tag=BANK_OF[g, h])
+            for g, first, count, bank in PIECES:
+                if first // HALF != h:
+                    continue
+                piece = slice(first, first + count)
+                scores.append(ps.tile([P, count], F32, name="scores%d_%d" % (g, first), tag=bank))
                 nc.tensor.matmul_mx(
-                    scores[g, h][:],
+                    scores[-1][:],
                     lhsT=q_codes[:, g * P : (g + 1) * P].bitcast(FP8X4),
                     lhsT_scale=q_scales[:, g * P : (g + 1) * P],
-                    rhs=key_words[:, slots].bitcast(FP8X4),
-                    rhs_scale=key_scales[:].bitcast(U8)[:, slots],
+                    rhs=key_words[:, piece].bitcast(FP8X4),
+                    rhs_scale=key_scales[:].bitcast(U8)[:, piece],
                     start=True,
                     stop=True,
                 )
 
         logits = [sb.tile([P, N], F32, name="logits%d" % g, align_bytes=64) for g in range(2)]
         gates = [sb.tile([P, N], F32, name="gates%d" % g, align_bytes=64) for g in range(2)]
-        half_sums = sb.tile([P, 2], F32, name="half_sums")
         total = [sb.tile([P, 1], F32, name="total%d" % g) for g in range(2)]
         inverse = [sb.tile([P, 1], F32, name="inverse%d" % g) for g in range(2)]
         result = [sb.tile([P, N], F32, name="result%d" % g, align_bytes=64) for g in range(2)]
-        for h in range(2):
-            slots = slice(h * HALF, (h + 1) * HALF)
-            for g in range(2):
-                nc.vector.tensor_tensor(logits[g][:, slots], scores[g, h][:], bias[:, slots], ALU.add)
-            nc.scalar.activation(gates[0][:, slots], logits[0][:, slots], ACT.Sigmoid, accum_out=half_sums[:, h : h + 1])
-        nc.scalar.activation(gates[1][:], logits[1][:], ACT.Sigmoid, accum_out=total[1][:])
-
-        nc.vector.tensor_scalar(total[0][:], half_sums[:, 0:1], half_sums[:, 1:2], 1.0 / GAIN, ALU.add, ALU.mult)
-        nc.vector.reciprocal(inverse[0][:], total[0][:])
-        nc.vector.tensor_scalar(result[0][:, :SCALE_SPLIT], gates[0][:, :SCALE_SPLIT], inverse[0][:], None, ALU.mult)
-        nc.scalar.activation(result[0][:, SCALE_SPLIT:], gates[0][:, SCALE_SPLIT:], ACT.Copy, scale=inverse[0][:])
-        nc.sync.dma_start(out[0, 0:P, :], result[0][:])
-        nc.vector.reciprocal(inverse[1][:], total[1][:])
-        nc.vector.tensor_scalar(result[1][:], gates[1][:], inverse[1][:], GAIN, ALU.mult, ALU.mult)
-        nc.sync.dma_start(out[0, P : 2 * P, :], result[1][:])
+        for i in ADD_ORDER:
+            g, first, count, bank = PIECES[i]
+            piece = slice(first, first + count)
+            nc.vector.tensor_tensor(logits[g][:, piece], scores[i][:], bias[:, piece], ALU.add)
+        for g in range(2):
+            nc.scalar.activation(gates[g][:], logits[g][:], ACT.Sigmoid, accum_out=total[g][:])
+        for g in range(2):
+            nc.vector.reciprocal(inverse[g][:], total[g][:])
+            nc.vector.tensor_scalar(result[g][:], gates[g][:], inverse[g][:], GAIN, ALU.mult, ALU.mult)
+            nc.sync.dma_start(out[0, g * P : (g + 1) * P, :], result[g][:])

@@ -25,16 +25,17 @@ BYTES = D * NQ * 4 + P * T * 4 + BLOCKS * T + T * 4 + P * (N // 16) * 2 + NQ * N
 
 BIAS_ROW = P - 1
 SCALE_ROW0 = 64 - BLOCKS
-ZERO_SPLIT = 1000
+ZERO_SPLIT = 600
+TURN_RUNS = ((0, 2), (2, 1), (3, 1))
 SPREAD_RUNS = ((0, 1), (1, 1), (2, 1), (3, 1))
 PIECES = (
-    (0, 0, 256, "turned1"),
+    (0, 0, 256, "turned3"),
     (1, 0, 256, "spread0"),
     (0, 256, 128, "spread1"),
     (0, 384, 128, "spread2"),
     (1, 256, 256, "spread3"),
 )
-ADD_ORDER = (0, 2, 3, 1, 4)
+SCALE_SPLIT = 344
 
 
 def tile_attend_nrm_sig_topk_kernel(tc, qT, k_words, k_scales, kb, offs, out):
@@ -85,14 +86,14 @@ def tile_attend_nrm_sig_topk_kernel(tc, qT, k_words, k_scales, kb, offs, out):
         bias_col = sb.tile([P, N // P], F32, name="bias_col", tag="q_raw", align_bytes=64)
         bias = sb.tile([P, N], F32, name="bias", align_bytes=64)
         for h in range(2):
-            slots = slice(h * HALF, (h + 1) * HALF)
             half_list = offsets[:, LIST_COLS * h : LIST_COLS * (h + 1)]
-            nc.vector.tensor_copy(kb_listed[:, slots], kb_pool[:].indirect(half_list))
-            turned = ps.tile([P, 2, P], F32, name="turned%d" % h, tag="turned%d" % h)
-            for u in range(2):
-                s = 2 * h + u
+            nc.vector.tensor_copy(kb_listed[:, h * HALF : (h + 1) * HALF], kb_pool[:].indirect(half_list))
+        for first, count in TURN_RUNS:
+            turned = ps.tile([P, count, P], F32, name="turned%d" % first, tag="turned%d" % first)
+            for u in range(count):
+                s = first + u
                 nc.tensor.transpose(turned[:, u, :], kb_listed[:, s * P : (s + 1) * P], ident[:])
-            nc.scalar.copy(bias_col[:, 2 * h : 2 * h + 2], turned[:, :, BIAS_ROW])
+            nc.scalar.copy(bias_col[:, first : first + count], turned[:, :, BIAS_ROW])
         q_codes = sb.tile([P, NQ], U32, name="q_codes", align_bytes=64)
         q_scales = sb.tile([P, NQ], U8, name="q_scales", align_bytes=64)
         nc.vector.quantize_mx(q_codes[:].bitcast(FP8X4), q_scales[:], q_bf[:].rearrange("p w t -> p (w t)"))
@@ -131,13 +132,22 @@ def tile_attend_nrm_sig_topk_kernel(tc, qT, k_words, k_scales, kb, offs, out):
         total = [sb.tile([P, 1], F32, name="total%d" % g) for g in range(2)]
         inverse = [sb.tile([P, 1], F32, name="inverse%d" % g) for g in range(2)]
         result = [sb.tile([P, N], F32, name="result%d" % g, align_bytes=64) for g in range(2)]
-        for i in ADD_ORDER:
-            g, first, count, bank = PIECES[i]
+        for (g, first, count, bank), sums in zip(PIECES, scores):
             piece = slice(first, first + count)
-            nc.vector.tensor_tensor(logits[g][:, piece], scores[i][:], bias[:, piece], ALU.add)
-        for g in range(2):
-            nc.scalar.activation(gates[g][:], logits[g][:], ACT.Sigmoid, accum_out=total[g][:])
-        for g in range(2):
-            nc.vector.reciprocal(inverse[g][:], total[g][:])
-            nc.vector.tensor_scalar(result[g][:], gates[g][:], inverse[g][:], GAIN, ALU.mult, ALU.mult)
-            nc.sync.dma_start(out[0, g * P : (g + 1) * P, :], result[g][:])
+            nc.vector.tensor_tensor(logits[g][:, piece], sums[:], bias[:, piece], ALU.add)
+        half_sums = sb.tile([P, 2], F32, name="half_sums")
+        for h in range(2):
+            slots = slice(h * HALF, (h + 1) * HALF)
+            nc.scalar.activation(gates[0][:, slots], logits[0][:, slots], ACT.Sigmoid, accum_out=half_sums[:, h : h + 1])
+        nc.scalar.activation(gates[1][:], logits[1][:], ACT.Sigmoid, accum_out=total[1][:])
+
+        nc.vector.tensor_scalar(total[0][:], half_sums[:, 0:1], half_sums[:, 1:2], 1.0 / GAIN, ALU.add, ALU.mult)
+        nc.vector.reciprocal(inverse[0][:], total[0][:])
+        nc.vector.tensor_scalar(result[0][:, :HALF], gates[0][:, :HALF], inverse[0][:], None, ALU.mult)
+        nc.sync.dma_start(out[0, 0:P, :HALF], result[0][:, :HALF])
+        nc.vector.tensor_scalar(result[0][:, HALF:SCALE_SPLIT], gates[0][:, HALF:SCALE_SPLIT], inverse[0][:], None, ALU.mult)
+        nc.scalar.activation(result[0][:, SCALE_SPLIT:], gates[0][:, SCALE_SPLIT:], ACT.Copy, scale=inverse[0][:])
+        nc.sync.dma_start(out[0, 0:P, HALF:], result[0][:, HALF:])
+        nc.vector.reciprocal(inverse[1][:], total[1][:])
+        nc.vector.tensor_scalar(result[1][:], gates[1][:], inverse[1][:], GAIN, ALU.mult, ALU.mult)
+        nc.sync.dma_start(out[0, P : 2 * P, :], result[1][:])

@@ -29,13 +29,13 @@ ZERO_SPLIT = 600
 TURN_RUNS = ((0, 2), (2, 1), (3, 1))
 SPREAD_RUNS = ((0, 1), (1, 1), (2, 1), (3, 1))
 PIECES = (
-    (0, 0, 256, "turned3"),
-    (1, 0, 256, "spread0"),
-    (0, 256, 128, "spread1"),
-    (0, 384, 128, "spread2"),
+    (0, 0, 256, "turned2"),
+    (1, 0, 128, "turned3"),
+    (0, 256, 128, "spread0"),
+    (0, 384, 128, "spread1"),
+    (1, 128, 128, "spread2"),
     (1, 256, 256, "spread3"),
 )
-SCALE_SPLIT = 344
 
 
 def tile_attend_nrm_sig_topk_kernel(tc, qT, k_words, k_scales, kb, offs, out):
@@ -109,23 +109,20 @@ def tile_attend_nrm_sig_topk_kernel(tc, qT, k_words, k_scales, kb, offs, out):
         key_words = sb.tile([P, N], U32, name="key_words", align_bytes=64)
         scores = []
         for h in range(2):
-            slots = slice(h * HALF, (h + 1) * HALF)
             half_list = offsets[:, LIST_COLS * h : LIST_COLS * (h + 1)]
-            nc.vector.tensor_copy(key_words[:, slots], word_pool[:].bitcast(U32).indirect(half_list))
-            for g, first, count, bank in PIECES:
-                if first // HALF != h:
-                    continue
-                piece = slice(first, first + count)
-                scores.append(ps.tile([P, count], F32, name="scores%d_%d" % (g, first), tag=bank))
-                nc.tensor.matmul_mx(
-                    scores[-1][:],
-                    lhsT=q_codes[:, g * P : (g + 1) * P].bitcast(FP8X4),
-                    lhsT_scale=q_scales[:, g * P : (g + 1) * P],
-                    rhs=key_words[:, piece].bitcast(FP8X4),
-                    rhs_scale=key_scales[:].bitcast(U8)[:, piece],
-                    start=True,
-                    stop=True,
-                )
+            nc.vector.tensor_copy(key_words[:, h * HALF : (h + 1) * HALF], word_pool[:].bitcast(U32).indirect(half_list))
+        for g, first, count, bank in PIECES:
+            piece = slice(first, first + count)
+            scores.append(ps.tile([P, count], F32, name="scores%d_%d" % (g, first), tag=bank))
+            nc.tensor.matmul_mx(
+                scores[-1][:],
+                lhsT=q_codes[:, g * P : (g + 1) * P].bitcast(FP8X4),
+                lhsT_scale=q_scales[:, g * P : (g + 1) * P],
+                rhs=key_words[:, piece].bitcast(FP8X4),
+                rhs_scale=key_scales[:].bitcast(U8)[:, piece],
+                start=True,
+                stop=True,
+            )
 
         logits = [sb.tile([P, N], F32, name="logits%d" % g, align_bytes=64) for g in range(2)]
         gates = [sb.tile([P, N], F32, name="gates%d" % g, align_bytes=64) for g in range(2)]
@@ -135,18 +132,18 @@ def tile_attend_nrm_sig_topk_kernel(tc, qT, k_words, k_scales, kb, offs, out):
         for (g, first, count, bank), sums in zip(PIECES, scores):
             piece = slice(first, first + count)
             nc.vector.tensor_tensor(logits[g][:, piece], sums[:], bias[:, piece], ALU.add)
-        half_sums = sb.tile([P, 2], F32, name="half_sums")
-        for h in range(2):
-            slots = slice(h * HALF, (h + 1) * HALF)
-            nc.scalar.activation(gates[0][:, slots], logits[0][:, slots], ACT.Sigmoid, accum_out=half_sums[:, h : h + 1])
+        first_pieces = [slice(first, first + count) for g, first, count, bank in PIECES if g == 0]
+        piece_sums = sb.tile([P, len(first_pieces)], F32, name="piece_sums")
+        scaled_sums = sb.tile([P, len(first_pieces)], F32, name="scaled_sums")
+        for i, piece in enumerate(first_pieces):
+            nc.scalar.activation(gates[0][:, piece], logits[0][:, piece], ACT.Sigmoid, accum_out=piece_sums[:, i : i + 1])
         nc.scalar.activation(gates[1][:], logits[1][:], ACT.Sigmoid, accum_out=total[1][:])
 
-        nc.vector.tensor_scalar(total[0][:], half_sums[:, 0:1], half_sums[:, 1:2], 1.0 / GAIN, ALU.add, ALU.mult)
+        nc.vector.tensor_scalar(scaled_sums[:], piece_sums[:], 1.0 / GAIN, None, ALU.mult, ALU.add, accum_out=total[0][:])
         nc.vector.reciprocal(inverse[0][:], total[0][:])
         nc.vector.tensor_scalar(result[0][:, :HALF], gates[0][:, :HALF], inverse[0][:], None, ALU.mult)
         nc.sync.dma_start(out[0, 0:P, :HALF], result[0][:, :HALF])
-        nc.vector.tensor_scalar(result[0][:, HALF:SCALE_SPLIT], gates[0][:, HALF:SCALE_SPLIT], inverse[0][:], None, ALU.mult)
-        nc.scalar.activation(result[0][:, SCALE_SPLIT:], gates[0][:, SCALE_SPLIT:], ACT.Copy, scale=inverse[0][:])
+        nc.scalar.activation(result[0][:, HALF:], gates[0][:, HALF:], ACT.Copy, scale=inverse[0][:])
         nc.sync.dma_start(out[0, 0:P, HALF:], result[0][:, HALF:])
         nc.vector.reciprocal(inverse[1][:], total[1][:])
         nc.vector.tensor_scalar(result[1][:], gates[1][:], inverse[1][:], GAIN, ALU.mult, ALU.mult)

@@ -25,7 +25,7 @@ BYTES = D * NQ * 4 + P * T * 4 + BLOCKS * T + T * 4 + P * (N // 16) * 2 + NQ * N
 
 BIAS_ROW = P - 1
 SCALE_ROW0 = 64 - BLOCKS
-ZERO_SPLIT = 600
+ZERO_SPLIT = 512
 TURN_RUNS = ((0, 2), (2, 1), (3, 1))
 SPREAD_RUNS = ((0, 1), (1, 1), (2, 1), (3, 1))
 PIECES = (
@@ -42,10 +42,11 @@ def tile_attend_nrm_sig_topk_kernel(tc, qT, k_words, k_scales, kb, offs, out):
     nc = tc.nc
     with ExitStack() as ctx:
         sb = ctx.enter_context(tc.tile_pool(name="sb", bufs=1))
+        reused = ctx.enter_context(tc.tile_pool(name="reused", bufs=1))
         ps = ctx.enter_context(tc.psum_pool(name="ps", bufs=1))
 
         offsets = sb.tile([P, N // 16], U16, name="offsets")
-        kb_pool = sb.tile([P, T], F32, name="kb_pool", align_bytes=64)
+        kb_pool = reused.tile([P, T], F32, name="kb_pool", align_bytes=64, offset=0)
         scale_pool = sb.tile([P, T // 4], I32, name="scale_pool", align_bytes=64)
         word_pool = sb.tile([P, T], I32, name="word_pool", align_bytes=64)
         q_raw = sb.tile([P, PACK, NQ], F32, name="q_raw", tag="q_raw", align_bytes=64)
@@ -58,12 +59,12 @@ def tile_attend_nrm_sig_topk_kernel(tc, qT, k_words, k_scales, kb, offs, out):
         nc.sync.dma_start(q_raw[:], qT[0].rearrange("(p j) w -> p j w", j=PACK))
         nc.sync.dma_start(word_pool[:], k_words[0].rearrange("p t r -> p (t r)").bitcast(I32))
 
-        nc.gpsimd.memset(scale_pool[SCALE_ROW0 + BLOCKS : P, :], 0)
-        nc.gpsimd.memset(kb_pool[0:BIAS_ROW, ZERO_SPLIT:T], 0.0)
-        nc.gpsimd.memset(key_scales[:], 0)
         make_identity(nc, ident[:])
-        nc.vector.memset(scale_pool[0:SCALE_ROW0, 0 : T // 4 - 1], 0)
-        nc.vector.memset(scale_pool[0:SCALE_ROW0, T // 4 - 1 : T // 4], 0)
+        nc.gpsimd.memset(key_scales[:], 0)
+        nc.gpsimd.memset(kb_pool[0:BIAS_ROW, ZERO_SPLIT:T], 0.0)
+        for rows in (slice(0, SCALE_ROW0), slice(SCALE_ROW0 + BLOCKS, P)):
+            nc.vector.memset(scale_pool[rows, 0 : T // 4 - 1], 0)
+            nc.vector.memset(scale_pool[rows, T // 4 - 1 : T // 4], 0)
         nc.vector.memset(kb_pool[0:BIAS_ROW, 0 : ZERO_SPLIT - 1], 0.0)
         nc.vector.memset(kb_pool[0:BIAS_ROW, ZERO_SPLIT - 1 : ZERO_SPLIT], 0.0)
 
@@ -95,7 +96,7 @@ def tile_attend_nrm_sig_topk_kernel(tc, qT, k_words, k_scales, kb, offs, out):
                 nc.tensor.transpose(turned[:, u, :], kb_listed[:, s * P : (s + 1) * P], ident[:])
             nc.scalar.copy(bias_col[:, first : first + count], turned[:, :, BIAS_ROW])
         q_codes = sb.tile([P, NQ], U32, name="q_codes", align_bytes=64)
-        q_scales = sb.tile([P, NQ], U8, name="q_scales", align_bytes=64)
+        q_scales = reused.tile([P, NQ], U8, name="q_scales", align_bytes=64, offset=4 * N)
         nc.vector.quantize_mx(q_codes[:].bitcast(FP8X4), q_scales[:], q_bf[:].rearrange("p w t -> p (w t)"))
 
         for first, count in SPREAD_RUNS:
@@ -106,7 +107,7 @@ def tile_attend_nrm_sig_topk_kernel(tc, qT, k_words, k_scales, kb, offs, out):
                 nc.tensor.transpose(spread[:, u * P : (u + 1) * P], column, ident[:])
             nc.scalar.copy(bias[:, first * P : (first + count) * P], spread[:])
 
-        key_words = sb.tile([P, N], U32, name="key_words", align_bytes=64)
+        key_words = reused.tile([P, N], U32, name="key_words", align_bytes=64, offset=0)
         scores = []
         for h in range(2):
             half_list = offsets[:, LIST_COLS * h : LIST_COLS * (h + 1)]

@@ -29,13 +29,16 @@ ZERO_SPLIT = 512
 TURN_RUNS = ((0, 2), (2, 1), (3, 1))
 SPREAD_RUNS = ((0, 1), (1, 1), (2, 1), (3, 1))
 PIECES = (
-    (0, 0, 256, "turned2"),
-    (1, 0, 128, "turned3"),
-    (0, 256, 128, "spread0"),
-    (0, 384, 128, "spread1"),
-    (1, 128, 128, "spread2"),
-    (1, 256, 256, "spread3"),
+    (0, 0, 128, "turned2"),
+    (0, 128, 128, "turned3"),
+    (1, 0, 128, "spread0"),
+    (0, 256, 128, "spread1"),
+    (0, 384, 128, "spread2"),
+    (1, 128, 128, "spread3"),
+    (1, 256, 128, "turned2"),
+    (1, 384, 128, "turned3"),
 )
+FIRST_GATES = ((0, 128), (128, 256), (256, 384), (384, 512))
 
 
 def tile_attend_nrm_sig_topk_kernel(tc, qT, k_words, k_scales, kb, offs, out):
@@ -108,15 +111,15 @@ def tile_attend_nrm_sig_topk_kernel(tc, qT, k_words, k_scales, kb, offs, out):
             nc.scalar.copy(bias[:, first * P : (first + count) * P], spread[:])
 
         key_words = reused.tile([P, N], U32, name="key_words", align_bytes=64, offset=0)
-        scores = []
         for h in range(2):
             half_list = offsets[:, LIST_COLS * h : LIST_COLS * (h + 1)]
             nc.vector.tensor_copy(key_words[:, h * HALF : (h + 1) * HALF], word_pool[:].bitcast(U32).indirect(half_list))
+        logits = [sb.tile([P, N], F32, name="logits%d" % g, align_bytes=64) for g in range(2)]
         for g, first, count, bank in PIECES:
             piece = slice(first, first + count)
-            scores.append(ps.tile([P, count], F32, name="scores%d_%d" % (g, first), tag=bank))
+            scores = ps.tile([P, count], F32, name="scores%d_%d" % (g, first), tag=bank)
             nc.tensor.matmul_mx(
-                scores[-1][:],
+                scores[:],
                 lhsT=q_codes[:, g * P : (g + 1) * P].bitcast(FP8X4),
                 lhsT_scale=q_scales[:, g * P : (g + 1) * P],
                 rhs=key_words[:, piece].bitcast(FP8X4),
@@ -124,16 +127,13 @@ def tile_attend_nrm_sig_topk_kernel(tc, qT, k_words, k_scales, kb, offs, out):
                 start=True,
                 stop=True,
             )
+            nc.vector.tensor_tensor(logits[g][:, piece], scores[:], bias[:, piece], ALU.add)
 
-        logits = [sb.tile([P, N], F32, name="logits%d" % g, align_bytes=64) for g in range(2)]
         gates = [sb.tile([P, N], F32, name="gates%d" % g, align_bytes=64) for g in range(2)]
         total = [sb.tile([P, 1], F32, name="total%d" % g) for g in range(2)]
         inverse = [sb.tile([P, 1], F32, name="inverse%d" % g) for g in range(2)]
         result = [sb.tile([P, N], F32, name="result%d" % g, align_bytes=64) for g in range(2)]
-        for (g, first, count, bank), sums in zip(PIECES, scores):
-            piece = slice(first, first + count)
-            nc.vector.tensor_tensor(logits[g][:, piece], sums[:], bias[:, piece], ALU.add)
-        first_pieces = [slice(first, first + count) for g, first, count, bank in PIECES if g == 0]
+        first_pieces = [slice(first, last) for first, last in FIRST_GATES]
         piece_sums = sb.tile([P, len(first_pieces)], F32, name="piece_sums")
         scaled_sums = sb.tile([P, len(first_pieces)], F32, name="scaled_sums")
         for i, piece in enumerate(first_pieces):

@@ -15,6 +15,7 @@ ACT = mybir.ActivationFunctionType
 
 P = 128
 PACK = 4
+WORD_BYTES = 4
 D, T, N, NQ = 512, 2048, 512, 256
 HALF = N // 2
 LIST_COLS = HALF // 16
@@ -26,19 +27,10 @@ BYTES = D * NQ * 4 + P * T * 4 + BLOCKS * T + T * 4 + P * (N // 16) * 2 + NQ * N
 BIAS_ROW = P - 1
 SCALE_ROW0 = 64 - BLOCKS
 ZERO_SPLIT = 512
+QUARTERS = N // P
 TURN_RUNS = ((0, 2), (2, 1), (3, 1))
-SPREAD_RUNS = ((0, 1), (1, 1), (2, 1), (3, 1))
-PIECES = (
-    (0, 0, 128, "turned2"),
-    (0, 128, 128, "turned3"),
-    (1, 0, 128, "spread0"),
-    (0, 256, 128, "spread1"),
-    (0, 384, 128, "spread2"),
-    (1, 128, 128, "spread3"),
-    (1, 256, 128, "turned2"),
-    (1, 384, 128, "turned3"),
-)
-FIRST_GATES = ((0, 128), (128, 256), (256, 384), (384, 512))
+PIECES = ((0, 0), (0, 1), (0, 2), (0, 3), (1, 0), (1, 1), (1, 2), (1, 3))
+SCORE_BANKS = ("turned2", "turned3", "spread0", "spread1", "spread2", "spread3")
 
 
 def tile_attend_nrm_sig_topk_kernel(tc, qT, k_words, k_scales, kb, offs, out):
@@ -51,16 +43,18 @@ def tile_attend_nrm_sig_topk_kernel(tc, qT, k_words, k_scales, kb, offs, out):
         offsets = sb.tile([P, N // 16], U16, name="offsets")
         kb_pool = reused.tile([P, T], F32, name="kb_pool", align_bytes=64, offset=0)
         scale_pool = sb.tile([P, T // 4], I32, name="scale_pool", align_bytes=64)
-        word_pool = sb.tile([P, T], I32, name="word_pool", align_bytes=64)
-        q_raw = sb.tile([P, PACK, NQ], F32, name="q_raw", tag="q_raw", align_bytes=64)
+        word_pool = reused.tile([P, T], I32, name="word_pool", align_bytes=64, offset=WORD_BYTES * T)
+        q_raw = sb.tile([P, 2, 2 * NQ], F32, name="q_raw", align_bytes=64)
         ident = sb.tile([P, P], F32, name="ident", align_bytes=64)
         key_scales = sb.tile([P, N // 4], I32, name="key_scales", align_bytes=64)
 
         nc.sync.dma_start(offsets[:], offs)
         nc.scalar.dma_start(scale_pool[SCALE_ROW0 : SCALE_ROW0 + BLOCKS, :], k_scales[0].bitcast(I32))
         nc.scalar.dma_start(kb_pool[BIAS_ROW:P, :], kb[0:1, :])
-        nc.sync.dma_start(q_raw[:], qT[0].rearrange("(p j) w -> p j w", j=PACK))
+        q_pairs = qT[0].rearrange("(p a b) w -> p a (b w)", a=2, b=2)
+        nc.sync.dma_start(q_raw[:, :, 0 : 3 * P], q_pairs[:, :, 0 : 3 * P])
         nc.sync.dma_start(word_pool[:], k_words[0].rearrange("p t r -> p (t r)").bitcast(I32))
+        nc.sync.dma_start(q_raw[:, :, 3 * P : 4 * P], q_pairs[:, :, 3 * P : 4 * P])
 
         make_identity(nc, ident[:])
         nc.gpsimd.memset(key_scales[:], 0)
@@ -80,14 +74,16 @@ def tile_attend_nrm_sig_topk_kernel(tc, qT, k_words, k_scales, kb, offs, out):
             rows = slice(SCALE_ROW0 + 4 * quad, SCALE_ROW0 + 4 * quad + 4)
             nc.sync.dma_start(key_scales[32 * quad : 32 * quad + 4, :], listed_scales[rows, :].bitcast(I32))
 
-        q_bf = sb.tile([P, NQ, PACK], BF16, name="q_bf", align_bytes=64)
-        nc.scalar.copy(
-            q_bf[:].rearrange("p (c i) t -> p c t i", i=4),
-            q_raw[:].rearrange("p t (c i) -> p c t i", i=4),
-        )
+        def cast(g, tag):
+            q_bf = sb.tile([P, P, PACK], BF16, name="q_bf%d" % g, tag=tag, align_bytes=64)
+            rows = q_raw[:].rearrange("p a (b g c i) -> p g c a b i", b=2, g=2, i=4)
+            nc.scalar.copy(q_bf[:].rearrange("p (c i) (a b) -> p c a b i", i=4, a=2), rows[:, g])
+            return q_bf[:].rearrange("p w t -> p (w t)")
 
-        kb_listed = sb.tile([P, N], F32, name="kb_listed", align_bytes=64)
-        bias_col = sb.tile([P, N // P], F32, name="bias_col", tag="q_raw", align_bytes=64)
+        first_bf = cast(0, "q_bf")
+
+        kb_listed = sb.tile([P, N], F32, name="kb_listed", tag="kb_listed", align_bytes=64)
+        bias_col = sb.tile([P, QUARTERS], F32, name="bias_col", align_bytes=64)
         bias = sb.tile([P, N], F32, name="bias", align_bytes=64)
         for h in range(2):
             half_list = offsets[:, LIST_COLS * h : LIST_COLS * (h + 1)]
@@ -98,30 +94,31 @@ def tile_attend_nrm_sig_topk_kernel(tc, qT, k_words, k_scales, kb, offs, out):
                 s = first + u
                 nc.tensor.transpose(turned[:, u, :], kb_listed[:, s * P : (s + 1) * P], ident[:])
             nc.scalar.copy(bias_col[:, first : first + count], turned[:, :, BIAS_ROW])
-        q_codes = sb.tile([P, NQ], U32, name="q_codes", align_bytes=64)
-        q_scales = reused.tile([P, NQ], U8, name="q_scales", align_bytes=64, offset=4 * N)
-        nc.vector.quantize_mx(q_codes[:].bitcast(FP8X4), q_scales[:], q_bf[:].rearrange("p w t -> p (w t)"))
+        second_bf = cast(1, "kb_listed")
+        q_codes = [sb.tile([P, P], U32, name="q_codes%d" % g, align_bytes=64) for g in range(2)]
+        q_scales = [
+            reused.tile([P, P], U8, name="q_scales%d" % g, align_bytes=64, offset=WORD_BYTES * (N, T)[g]) for g in range(2)
+        ]
+        nc.vector.quantize_mx(q_codes[0][:].bitcast(FP8X4), q_scales[0][:], first_bf)
 
-        for first, count in SPREAD_RUNS:
-            spread = ps.tile([P, count * P], F32, name="spread%d" % first, tag="spread%d" % first)
-            for u in range(count):
-                s = first + u
-                column = bias_col[:, s : s + 1].to_broadcast([P, P])
-                nc.tensor.transpose(spread[:, u * P : (u + 1) * P], column, ident[:])
-            nc.scalar.copy(bias[:, first * P : (first + count) * P], spread[:])
+        for s in range(QUARTERS):
+            spread = ps.tile([P, P], F32, name="spread%d" % s, tag="spread%d" % s)
+            nc.tensor.transpose(spread[:], bias_col[:, s : s + 1].to_broadcast([P, P]), ident[:])
+            nc.scalar.copy(bias[:, s * P : (s + 1) * P], spread[:])
 
         key_words = reused.tile([P, N], U32, name="key_words", align_bytes=64, offset=0)
         for h in range(2):
             half_list = offsets[:, LIST_COLS * h : LIST_COLS * (h + 1)]
             nc.vector.tensor_copy(key_words[:, h * HALF : (h + 1) * HALF], word_pool[:].bitcast(U32).indirect(half_list))
+        nc.vector.quantize_mx(q_codes[1][:].bitcast(FP8X4), q_scales[1][:], second_bf)
         logits = [sb.tile([P, N], F32, name="logits%d" % g, align_bytes=64) for g in range(2)]
-        for g, first, count, bank in PIECES:
-            piece = slice(first, first + count)
-            scores = ps.tile([P, count], F32, name="scores%d_%d" % (g, first), tag=bank)
+        for i, (g, s) in enumerate(PIECES):
+            piece = slice(s * P, (s + 1) * P)
+            scores = ps.tile([P, P], F32, name="scores%d_%d" % (g, s), tag=SCORE_BANKS[i % len(SCORE_BANKS)])
             nc.tensor.matmul_mx(
                 scores[:],
-                lhsT=q_codes[:, g * P : (g + 1) * P].bitcast(FP8X4),
-                lhsT_scale=q_scales[:, g * P : (g + 1) * P],
+                lhsT=q_codes[g][:].bitcast(FP8X4),
+                lhsT_scale=q_scales[g][:],
                 rhs=key_words[:, piece].bitcast(FP8X4),
                 rhs_scale=key_scales[:].bitcast(U8)[:, piece],
                 start=True,
@@ -133,11 +130,11 @@ def tile_attend_nrm_sig_topk_kernel(tc, qT, k_words, k_scales, kb, offs, out):
         total = [sb.tile([P, 1], F32, name="total%d" % g) for g in range(2)]
         inverse = [sb.tile([P, 1], F32, name="inverse%d" % g) for g in range(2)]
         result = [sb.tile([P, N], F32, name="result%d" % g, align_bytes=64) for g in range(2)]
-        first_pieces = [slice(first, last) for first, last in FIRST_GATES]
-        piece_sums = sb.tile([P, len(first_pieces)], F32, name="piece_sums")
-        scaled_sums = sb.tile([P, len(first_pieces)], F32, name="scaled_sums")
-        for i, piece in enumerate(first_pieces):
-            nc.scalar.activation(gates[0][:, piece], logits[0][:, piece], ACT.Sigmoid, accum_out=piece_sums[:, i : i + 1])
+        piece_sums = sb.tile([P, QUARTERS], F32, name="piece_sums")
+        scaled_sums = sb.tile([P, QUARTERS], F32, name="scaled_sums")
+        for s in range(QUARTERS):
+            piece = slice(s * P, (s + 1) * P)
+            nc.scalar.activation(gates[0][:, piece], logits[0][:, piece], ACT.Sigmoid, accum_out=piece_sums[:, s : s + 1])
         nc.scalar.activation(gates[1][:], logits[1][:], ACT.Sigmoid, accum_out=total[1][:])
 
         nc.vector.tensor_scalar(scaled_sums[:], piece_sums[:], 1.0 / GAIN, None, ALU.mult, ALU.add, accum_out=total[0][:])

@@ -15,7 +15,6 @@ ACT = mybir.ActivationFunctionType
 
 P = 128
 PACK = 4
-WORD_BYTES = 4
 D, T, N, NQ = 512, 2048, 512, 256
 HALF = N // 2
 LIST_COLS = HALF // 16
@@ -24,9 +23,9 @@ GAIN = 2.5
 FLOPS = 2 * NQ * N * D
 BYTES = D * NQ * 4 + P * T * 4 + BLOCKS * T + T * 4 + P * (N // 16) * 2 + NQ * N * 4
 
-BIAS_ROW = P - 1
-SCALE_ROW0 = 64 - BLOCKS
-ZERO_SPLIT = 512
+BIAS_ROWS = (63, 127)
+ZERO_SPLIT = 832
+SCALE_STEP = P // BLOCKS
 QUARTERS = N // P
 TURN_RUNS = ((0, 2), (2, 1), (3, 1))
 PIECES = ((0, 0), (0, 1), (0, 2), (0, 3), (1, 0), (1, 1), (1, 2), (1, 3))
@@ -37,68 +36,79 @@ def tile_attend_nrm_sig_topk_kernel(tc, qT, k_words, k_scales, kb, offs, out):
     nc = tc.nc
     with ExitStack() as ctx:
         sb = ctx.enter_context(tc.tile_pool(name="sb", bufs=1))
-        reused = ctx.enter_context(tc.tile_pool(name="reused", bufs=1))
         ps = ctx.enter_context(tc.psum_pool(name="ps", bufs=1))
 
         offsets = sb.tile([P, N // 16], U16, name="offsets")
-        kb_pool = reused.tile([P, T], F32, name="kb_pool", align_bytes=64, offset=0)
-        scale_pool = sb.tile([P, T // 4], I32, name="scale_pool", align_bytes=64)
-        word_pool = reused.tile([P, T], I32, name="word_pool", align_bytes=64, offset=WORD_BYTES * T)
+        kb_pool = sb.tile([P, T], F32, name="kb_pool", align_bytes=64)
+        scale_pool = sb.tile([P, T // 4], I32, name="scale_pool", tag="scale_pool", align_bytes=64)
+        word_pool = sb.tile([P, T], I32, name="word_pool", align_bytes=64)
         q_raw = sb.tile([P, 2, 2 * NQ], F32, name="q_raw", align_bytes=64)
         ident = sb.tile([P, P], F32, name="ident", align_bytes=64)
         key_scales = sb.tile([P, N // 4], I32, name="key_scales", align_bytes=64)
 
-        nc.sync.dma_start(offsets[:], offs)
-        nc.scalar.dma_start(scale_pool[SCALE_ROW0 : SCALE_ROW0 + BLOCKS, :], k_scales[0].bitcast(I32))
-        nc.scalar.dma_start(kb_pool[BIAS_ROW:P, :], kb[0:1, :])
         q_pairs = qT[0].rearrange("(p a b) w -> p a (b w)", a=2, b=2)
-        nc.sync.dma_start(q_raw[:, :, 0 : 3 * P], q_pairs[:, :, 0 : 3 * P])
+        nc.sync.dma_start(q_raw[:, 0, 0 : 3 * P], q_pairs[:, 0, 0 : 3 * P])
+        nc.sync.dma_start(offsets[:], offs)
+        for h, (row, queue) in enumerate(zip(BIAS_ROWS, (nc.scalar, nc.sync))):
+            tokens = slice(h * T // 2, (h + 1) * T // 2)
+            queue.dma_start(kb_pool[row : row + 1, tokens], kb[0:1, tokens])
+        nc.vector.memset(scale_pool[:, 0 : T // 8 - 1], 0)
+        nc.vector.memset(scale_pool[:, T // 8 - 1 : T // 8], 0)
+        nc.gpsimd.memset(scale_pool[:, T // 8 : T // 4], 0)
+        nc.sync.dma_start(scale_pool[0:P:SCALE_STEP, :], k_scales[0].bitcast(I32))
+        nc.sync.dma_start(q_raw[:, 1, 0 : 3 * P], q_pairs[:, 1, 0 : 3 * P])
         nc.sync.dma_start(word_pool[:], k_words[0].rearrange("p t r -> p (t r)").bitcast(I32))
         nc.sync.dma_start(q_raw[:, :, 3 * P : 4 * P], q_pairs[:, :, 3 * P : 4 * P])
 
         make_identity(nc, ident[:])
+        nc.gpsimd.memset(kb_pool[0 : BIAS_ROWS[1], T // 2 : T], 0.0)
+        nc.gpsimd.memset(kb_pool[P // 2 : P, ZERO_SPLIT : T // 2], 0.0)
         nc.gpsimd.memset(key_scales[:], 0)
-        nc.gpsimd.memset(kb_pool[0:BIAS_ROW, ZERO_SPLIT:T], 0.0)
-        for rows in (slice(0, SCALE_ROW0), slice(SCALE_ROW0 + BLOCKS, P)):
-            nc.vector.memset(scale_pool[rows, 0 : T // 4 - 1], 0)
-            nc.vector.memset(scale_pool[rows, T // 4 - 1 : T // 4], 0)
-        nc.vector.memset(kb_pool[0:BIAS_ROW, 0 : ZERO_SPLIT - 1], 0.0)
-        nc.vector.memset(kb_pool[0:BIAS_ROW, ZERO_SPLIT - 1 : ZERO_SPLIT], 0.0)
+        for rows, width in ((slice(0, BIAS_ROWS[0]), T // 2), (slice(P // 2, P), ZERO_SPLIT)):
+            nc.vector.memset(kb_pool[rows, 0 : width - 1], 0.0)
+            nc.vector.memset(kb_pool[rows, width - 1 : width], 0.0)
 
         unread = sb.tile([P, 1], F32, name="unread")
-        nc.scalar.activation(unread[0:BIAS_ROW, :], kb_pool[0:BIAS_ROW, 0:1], ACT.Sigmoid)
+        nc.scalar.activation(unread[:], ident[:, 0:1], ACT.Sigmoid)
 
         listed_scales = sb.tile([P, N], U8, name="listed_scales", align_bytes=64)
         nc.vector.tensor_copy(listed_scales[:], scale_pool[:].bitcast(U8).indirect(offsets[:]))
+        moves = []
         for quad in range(4):
-            rows = slice(SCALE_ROW0 + 4 * quad, SCALE_ROW0 + 4 * quad + 4)
-            nc.sync.dma_start(key_scales[32 * quad : 32 * quad + 4, :], listed_scales[rows, :].bitcast(I32))
+            rows = slice(32 * quad, 32 * quad + 32, SCALE_STEP)
+            moves.append((key_scales[32 * quad : 32 * quad + 4, :], listed_scales[rows, :].bitcast(I32)))
+        for move in moves[:2]:
+            nc.sync.dma_start(*move)
 
-        def cast(g, tag):
+        def cast(g, tag, copy):
             q_bf = sb.tile([P, P, PACK], BF16, name="q_bf%d" % g, tag=tag, align_bytes=64)
             rows = q_raw[:].rearrange("p a (b g c i) -> p g c a b i", b=2, g=2, i=4)
-            nc.scalar.copy(q_bf[:].rearrange("p (c i) (a b) -> p c a b i", i=4, a=2), rows[:, g])
+            copy(q_bf[:].rearrange("p (c i) (a b) -> p c a b i", i=4, a=2), rows[:, g])
             return q_bf[:].rearrange("p w t -> p (w t)")
 
-        first_bf = cast(0, "q_bf")
+        first_bf = cast(0, "scale_pool", nc.vector.tensor_copy)
 
         kb_listed = sb.tile([P, N], F32, name="kb_listed", tag="kb_listed", align_bytes=64)
         bias_col = sb.tile([P, QUARTERS], F32, name="bias_col", align_bytes=64)
+        both = sb.tile([P, QUARTERS, 2], F32, name="both")
         bias = sb.tile([P, N], F32, name="bias", align_bytes=64)
         for h in range(2):
             half_list = offsets[:, LIST_COLS * h : LIST_COLS * (h + 1)]
-            nc.vector.tensor_copy(kb_listed[:, h * HALF : (h + 1) * HALF], kb_pool[:].indirect(half_list))
+            nc.scalar.activation(kb_listed[:, h * HALF : (h + 1) * HALF], kb_pool[:].indirect(half_list), ACT.Copy)
+        for move in moves[2:]:
+            nc.scalar.dma_start(*move)
         for first, count in TURN_RUNS:
             turned = ps.tile([P, count, P], F32, name="turned%d" % first, tag="turned%d" % first)
             for u in range(count):
                 s = first + u
                 nc.tensor.transpose(turned[:, u, :], kb_listed[:, s * P : (s + 1) * P], ident[:])
-            nc.scalar.copy(bias_col[:, first : first + count], turned[:, :, BIAS_ROW])
-        second_bf = cast(1, "kb_listed")
+            for u in range(count):
+                s = first + u
+                halves = turned[:, u, BIAS_ROWS[0] : P : P // 2]
+                nc.scalar.activation(both[:, s, :], halves, ACT.Copy, accum_out=bias_col[:, s : s + 1])
+        second_bf = cast(1, "kb_listed", nc.scalar.copy)
         q_codes = [sb.tile([P, P], U32, name="q_codes%d" % g, align_bytes=64) for g in range(2)]
-        q_scales = [
-            reused.tile([P, P], U8, name="q_scales%d" % g, align_bytes=64, offset=WORD_BYTES * (N, T)[g]) for g in range(2)
-        ]
+        q_scales = [sb.tile([P, P], U8, name="q_scales%d" % g, align_bytes=64) for g in range(2)]
         nc.vector.quantize_mx(q_codes[0][:].bitcast(FP8X4), q_scales[0][:], first_bf)
 
         for s in range(QUARTERS):
@@ -106,7 +116,7 @@ def tile_attend_nrm_sig_topk_kernel(tc, qT, k_words, k_scales, kb, offs, out):
             nc.tensor.transpose(spread[:], bias_col[:, s : s + 1].to_broadcast([P, P]), ident[:])
             nc.scalar.copy(bias[:, s * P : (s + 1) * P], spread[:])
 
-        key_words = reused.tile([P, N], U32, name="key_words", align_bytes=64, offset=0)
+        key_words = sb.tile([P, N], U32, name="key_words", align_bytes=64)
         for h in range(2):
             half_list = offsets[:, LIST_COLS * h : LIST_COLS * (h + 1)]
             nc.vector.tensor_copy(key_words[:, h * HALF : (h + 1) * HALF], word_pool[:].bitcast(U32).indirect(half_list))

@@ -24,7 +24,7 @@ FLOPS = 2 * NQ * N * D
 BYTES = D * NQ * 4 + P * T * 4 + BLOCKS * T + T * 4 + P * (N // 16) * 2 + NQ * N * 4
 
 BIAS_ROWS = (63, 127)
-ZERO_SPLIT = 832
+BIAS_CUT = 768
 SCALE_STEP = P // BLOCKS
 QUARTERS = N // P
 TURN_RUNS = ((0, 2), (2, 1), (3, 1))
@@ -49,27 +49,25 @@ def tile_attend_nrm_sig_topk_kernel(tc, qT, k_words, k_scales, kb, offs, out):
         q_pairs = qT[0].rearrange("(p a b) w -> p a (b w)", a=2, b=2)
         nc.sync.dma_start(q_raw[:, 0, 0 : 3 * P], q_pairs[:, 0, 0 : 3 * P])
         nc.sync.dma_start(offsets[:], offs)
-        for h, (row, queue) in enumerate(zip(BIAS_ROWS, (nc.scalar, nc.sync))):
-            tokens = slice(h * T // 2, (h + 1) * T // 2)
-            queue.dma_start(kb_pool[row : row + 1, tokens], kb[0:1, tokens])
-        nc.vector.memset(scale_pool[:, 0 : T // 8 - 1], 0)
-        nc.vector.memset(scale_pool[:, T // 8 - 1 : T // 8], 0)
-        nc.gpsimd.memset(scale_pool[:, T // 8 : T // 4], 0)
+        for row, tokens in zip(BIAS_ROWS, (slice(0, BIAS_CUT), slice(BIAS_CUT, T))):
+            nc.sync.dma_start(kb_pool[row : row + 1, tokens], kb[0:1, tokens])
+        nc.gpsimd.memset(scale_pool[:], 0)
         nc.sync.dma_start(scale_pool[0:P:SCALE_STEP, :], k_scales[0].bitcast(I32))
         nc.sync.dma_start(q_raw[:, 1, 0 : 3 * P], q_pairs[:, 1, 0 : 3 * P])
         nc.sync.dma_start(word_pool[:], k_words[0].rearrange("p t r -> p (t r)").bitcast(I32))
         nc.sync.dma_start(q_raw[:, :, 3 * P : 4 * P], q_pairs[:, :, 3 * P : 4 * P])
 
         make_identity(nc, ident[:])
-        nc.gpsimd.memset(kb_pool[0 : BIAS_ROWS[1], T // 2 : T], 0.0)
-        nc.gpsimd.memset(kb_pool[P // 2 : P, ZERO_SPLIT : T // 2], 0.0)
+        nc.gpsimd.memset(kb_pool[0 : BIAS_ROWS[1], BIAS_CUT:T], 0.0)
         nc.gpsimd.memset(key_scales[:], 0)
-        for rows, width in ((slice(0, BIAS_ROWS[0]), T // 2), (slice(P // 2, P), ZERO_SPLIT)):
-            nc.vector.memset(kb_pool[rows, 0 : width - 1], 0.0)
-            nc.vector.memset(kb_pool[rows, width - 1 : width], 0.0)
+        zero = sb.tile([P, 1], F32, name="zero")
+        nc.vector.memset(zero[:], 0.0)
+        for rows in (slice(0, BIAS_ROWS[0]), slice(BIAS_ROWS[0] + 1, P)):
+            nc.vector.memset(kb_pool[rows, 0 : BIAS_CUT - 1], 0.0)
+            nc.vector.memset(kb_pool[rows, BIAS_CUT - 1 : BIAS_CUT], 0.0)
 
         unread = sb.tile([P, 1], F32, name="unread")
-        nc.scalar.activation(unread[:], ident[:, 0:1], ACT.Sigmoid)
+        nc.scalar.activation(unread[:], zero[:], ACT.Sigmoid)
 
         listed_scales = sb.tile([P, N], U8, name="listed_scales", align_bytes=64)
         nc.vector.tensor_copy(listed_scales[:], scale_pool[:].bitcast(U8).indirect(offsets[:]))

@@ -29,7 +29,7 @@ SCALE_STEP = P // BLOCKS
 QUARTERS = N // P
 TURN_RUNS = ((0, 2), (2, 1), (3, 1))
 PIECES = ((0, 0), (0, 1), (0, 2), (0, 3), (1, 0), (1, 1), (1, 2), (1, 3))
-SCORE_BANKS = ("turned2", "turned3", "spread0", "spread1", "spread2", "spread3")
+SCORE_BANKS = ("turned2", "turned3", "turned0", "last", "spread0", "spread1", "spread2", "spread3")
 
 
 def tile_attend_nrm_sig_topk_kernel(tc, qT, k_words, k_scales, kb, offs, out):
@@ -50,8 +50,10 @@ def tile_attend_nrm_sig_topk_kernel(tc, qT, k_words, k_scales, kb, offs, out):
         nc.sync.dma_start(q_raw[:, 0, 0 : 3 * P], q_pairs[:, 0, 0 : 3 * P])
         nc.sync.dma_start(offsets[:], offs)
         for row, tokens in zip(BIAS_ROWS, (slice(0, BIAS_CUT), slice(BIAS_CUT, T))):
-            nc.sync.dma_start(kb_pool[row : row + 1, tokens], kb[0:1, tokens])
-        nc.gpsimd.memset(scale_pool[:], 0)
+            nc.scalar.dma_start(kb_pool[row : row + 1, tokens], kb[0:1, tokens])
+        nc.vector.memset(scale_pool[:, 0 : T // 8 - 1], 0)
+        nc.vector.memset(scale_pool[:, T // 8 - 1 : T // 8], 0)
+        nc.gpsimd.memset(scale_pool[:, T // 8 : T // 4], 0)
         nc.sync.dma_start(scale_pool[0:P:SCALE_STEP, :], k_scales[0].bitcast(I32))
         nc.sync.dma_start(q_raw[:, 1, 0 : 3 * P], q_pairs[:, 1, 0 : 3 * P])
         nc.sync.dma_start(word_pool[:], k_words[0].rearrange("p t r -> p (t r)").bitcast(I32))

@@ -95,8 +95,9 @@ def tile_attend_nrm_sig_topk_kernel(tc, qT, k_words, k_scales, kb, offs, out):
         for h in range(2):
             half_list = offsets[:, LIST_COLS * h : LIST_COLS * (h + 1)]
             nc.scalar.activation(kb_listed[:, h * HALF : (h + 1) * HALF], kb_pool[:].indirect(half_list), ACT.Copy)
-        for move in moves[2:]:
-            nc.scalar.dma_start(*move)
+            if h == 0:
+                for move in moves[2:]:
+                    nc.scalar.dma_start(*move)
         for first, count in TURN_RUNS:
             turned = ps.tile([P, count, P], F32, name="turned%d" % first, tag="turned%d" % first)
             for u in range(count):
@@ -117,9 +118,9 @@ def tile_attend_nrm_sig_topk_kernel(tc, qT, k_words, k_scales, kb, offs, out):
             nc.scalar.copy(bias[:, s * P : (s + 1) * P], spread[:])
 
         key_words = sb.tile([P, N], U32, name="key_words", align_bytes=64)
-        for h in range(2):
-            half_list = offsets[:, LIST_COLS * h : LIST_COLS * (h + 1)]
-            nc.vector.tensor_copy(key_words[:, h * HALF : (h + 1) * HALF], word_pool[:].bitcast(U32).indirect(half_list))
+        for first, last in ((0, 1), (1, 2), (2, 3), (3, 4)):
+            part_list = offsets[:, P // 16 * first : P // 16 * last]
+            nc.vector.tensor_copy(key_words[:, first * P : last * P], word_pool[:].bitcast(U32).indirect(part_list))
         nc.vector.quantize_mx(q_codes[1][:].bitcast(FP8X4), q_scales[1][:], second_bf)
         logits = [sb.tile([P, N], F32, name="logits%d" % g, align_bytes=64) for g in range(2)]
         for i, (g, s) in enumerate(PIECES):

@@ -107,7 +107,11 @@ def tile_attend_nrm_sig_topk_kernel(tc, qT, k_words, k_scales, kb, offs, out):
                 s = first + u
                 halves = turned[:, u, BIAS_ROWS[0] : P : P // 2]
                 nc.scalar.activation(both[:, s, :], halves, ACT.Copy, accum_out=bias_col[:, s : s + 1])
-        second_bf = cast(1, "kb_listed", nc.scalar.copy)
+        second_tile = sb.tile([P, P, PACK], BF16, name="second_tile", tag="kb_listed", align_bytes=64)
+        by_row = q_raw[:].rearrange("p a (b g c i) -> p g b c a i", b=2, g=2, i=4)
+        for b in range(2):
+            nc.scalar.copy(second_tile[:].rearrange("p (c i) (a b) -> p b c a i", i=4, a=2)[:, b], by_row[:, 1, b])
+        second_bf = second_tile[:].rearrange("p w t -> p (w t)")
         q_codes = [sb.tile([P, P], U32, name="q_codes%d" % g, align_bytes=64) for g in range(2)]
         q_scales = [sb.tile([P, P], U8, name="q_scales%d" % g, align_bytes=64) for g in range(2)]
         nc.vector.quantize_mx(q_codes[0][:].bitcast(FP8X4), q_scales[0][:], first_bf)

@@ -24,8 +24,9 @@ FLOPS = 2 * NQ * N * D
 BYTES = D * NQ * 4 + P * T * 4 + BLOCKS * T + T * 4 + P * (N // 16) * 2 + NQ * N * 4
 
 BIAS_ROWS = (63, 127)
-BIAS_CUT = 768
+BIAS_CUT = 832
 SCALE_STEP = P // BLOCKS
+SCALE_CUT = 368
 QUARTERS = N // P
 TURN_RUNS = ((0, 2), (2, 1), (3, 1))
 PIECES = ((0, 0), (0, 1), (0, 2), (0, 3), (1, 0), (1, 1), (1, 2), (1, 3))
@@ -40,7 +41,7 @@ def tile_attend_nrm_sig_topk_kernel(tc, qT, k_words, k_scales, kb, offs, out):
 
         offsets = sb.tile([P, N // 16], U16, name="offsets")
         kb_pool = sb.tile([P, T], F32, name="kb_pool", align_bytes=64)
-        scale_pool = sb.tile([P, T // 4], I32, name="scale_pool", tag="scale_pool", align_bytes=64)
+        scale_pool = sb.tile([P, T // 4 + 1], I32, name="scale_pool", tag="scale_pool", align_bytes=64)
         word_pool = sb.tile([P, T], I32, name="word_pool", align_bytes=64)
         q_raw = sb.tile([P, 2, 2 * NQ], F32, name="q_raw", align_bytes=64)
         ident = sb.tile([P, P], F32, name="ident", align_bytes=64)
@@ -51,10 +52,9 @@ def tile_attend_nrm_sig_topk_kernel(tc, qT, k_words, k_scales, kb, offs, out):
         nc.sync.dma_start(offsets[:], offs)
         for row, tokens in zip(BIAS_ROWS, (slice(0, BIAS_CUT), slice(BIAS_CUT, T))):
             nc.scalar.dma_start(kb_pool[row : row + 1, tokens], kb[0:1, tokens])
-        nc.vector.memset(scale_pool[:, 0 : T // 8 - 1], 0)
-        nc.vector.memset(scale_pool[:, T // 8 - 1 : T // 8], 0)
-        nc.gpsimd.memset(scale_pool[:, T // 8 : T // 4], 0)
-        nc.sync.dma_start(scale_pool[0:P:SCALE_STEP, :], k_scales[0].bitcast(I32))
+        nc.vector.memset(scale_pool[:, SCALE_CUT:], 0)
+        nc.gpsimd.memset(scale_pool[:, 0:SCALE_CUT], 0)
+        nc.sync.dma_start(scale_pool[0:P:SCALE_STEP, 0 : T // 4], k_scales[0].bitcast(I32))
         nc.sync.dma_start(q_raw[:, 1, 0 : 3 * P], q_pairs[:, 1, 0 : 3 * P])
         nc.sync.dma_start(word_pool[:], k_words[0].rearrange("p t r -> p (t r)").bitcast(I32))
         nc.sync.dma_start(q_raw[:, :, 3 * P : 4 * P], q_pairs[:, :, 3 * P : 4 * P])
@@ -72,7 +72,7 @@ def tile_attend_nrm_sig_topk_kernel(tc, qT, k_words, k_scales, kb, offs, out):
         nc.scalar.activation(unread[:], zero[:], ACT.Sigmoid)
 
         listed_scales = sb.tile([P, N], U8, name="listed_scales", align_bytes=64)
-        nc.vector.tensor_copy(listed_scales[:], scale_pool[:].bitcast(U8).indirect(offsets[:]))
+        nc.vector.tensor_copy(listed_scales[:], scale_pool[:, 0 : T // 4].bitcast(U8).indirect(offsets[:]))
         moves = []
         for quad in range(4):
             rows = slice(32 * quad, 32 * quad + 32, SCALE_STEP)

@@ -37,11 +37,12 @@ def tile_attend_nrm_sig_topk_kernel(tc, qT, k_words, k_scales, kb, offs, out):
     nc = tc.nc
     with ExitStack() as ctx:
         sb = ctx.enter_context(tc.tile_pool(name="sb", bufs=1))
+        shared = ctx.enter_context(tc.tile_pool(name="shared", bufs=1))
         ps = ctx.enter_context(tc.psum_pool(name="ps", bufs=1))
 
         offsets = sb.tile([P, N // 16], U16, name="offsets")
         kb_pool = sb.tile([P, T], F32, name="kb_pool", align_bytes=64)
-        scale_pool = sb.tile([P, T // 4 + 1], I32, name="scale_pool", tag="scale_pool", align_bytes=64)
+        scale_pool = shared.tile([P, T // 4 + 1], I32, name="scale_pool", offset=0, align_bytes=64)
         word_pool = sb.tile([P, T], I32, name="word_pool", align_bytes=64)
         q_raw = sb.tile([P, 2, 2 * NQ], F32, name="q_raw", align_bytes=64)
         ident = sb.tile([P, P], F32, name="ident", align_bytes=64)
@@ -80,29 +81,31 @@ def tile_attend_nrm_sig_topk_kernel(tc, qT, k_words, k_scales, kb, offs, out):
         for move in moves[:2]:
             nc.sync.dma_start(*move)
 
-        def cast(g, tag, copy):
-            q_bf = sb.tile([P, P, PACK], BF16, name="q_bf%d" % g, tag=tag, align_bytes=64)
+        def cast(g, copy):
+            q_bf = shared.tile([P, P, PACK], BF16, name="q_bf%d" % g, offset=0, align_bytes=64)
             rows = q_raw[:].rearrange("p a (b g c i) -> p g c a b i", b=2, g=2, i=4)
             copy(q_bf[:].rearrange("p (c i) (a b) -> p c a b i", i=4, a=2), rows[:, g])
             return q_bf[:].rearrange("p w t -> p (w t)")
 
-        first_bf = cast(0, "scale_pool", nc.vector.tensor_copy)
+        first_bf = cast(0, nc.vector.tensor_copy)
 
-        kb_listed = sb.tile([P, N], F32, name="kb_listed", tag="kb_listed", align_bytes=64)
+        kb_listed = sb.tile([P, N - P], F32, name="kb_listed", tag="kb_listed", align_bytes=64)
+        kb_last = shared.tile([P, P], F32, name="kb_last", offset=2 * P * PACK, align_bytes=64)
+        listed = [kb_listed[:, s * P : (s + 1) * P] for s in range(QUARTERS - 1)] + [kb_last[:]]
         bias_col = sb.tile([P, QUARTERS], F32, name="bias_col", align_bytes=64)
         both = sb.tile([P, QUARTERS, 2], F32, name="both")
         bias = sb.tile([P, N], F32, name="bias", align_bytes=64)
-        for h in range(2):
-            half_list = offsets[:, LIST_COLS * h : LIST_COLS * (h + 1)]
-            nc.scalar.activation(kb_listed[:, h * HALF : (h + 1) * HALF], kb_pool[:].indirect(half_list), ACT.Copy)
-            if h == 0:
-                for move in moves[2:]:
-                    nc.scalar.dma_start(*move)
+        for first, last in ((0, 2), (2, 3)):
+            part_list = offsets[:, P // 16 * first : P // 16 * last]
+            nc.scalar.activation(kb_listed[:, first * P : last * P], kb_pool[:].indirect(part_list), ACT.Copy)
+        for move in moves[2:]:
+            nc.scalar.dma_start(*move)
+        nc.scalar.activation(kb_last[:], kb_pool[:].indirect(offsets[:, P // 16 * (QUARTERS - 1) :]), ACT.Copy)
         for first, count in TURN_RUNS:
             turned = ps.tile([P, count, P], F32, name="turned%d" % first, tag="turned%d" % first)
             for u in range(count):
                 s = first + u
-                nc.tensor.transpose(turned[:, u, :], kb_listed[:, s * P : (s + 1) * P], ident[:])
+                nc.tensor.transpose(turned[:, u, :], listed[s], ident[:])
             for u in range(count):
                 s = first + u
                 halves = turned[:, u, BIAS_ROWS[0] : P : P // 2]

from contextlib import ExitStack

import concourse.mybir as mybir
from concourse.masks import make_identity

F32 = mybir.dt.float32
BF16 = mybir.dt.bfloat16
I32 = mybir.dt.int32
U32 = mybir.dt.uint32
U16 = mybir.dt.uint16
U8 = mybir.dt.uint8
FP8X4 = mybir.dt.float8_e4m3fn_x4
ALU = mybir.AluOpType
ACT = mybir.ActivationFunctionType

P = 128
PACK = 4
D, T, N, NQ = 512, 2048, 512, 256
HALF = N // 2
LIST_COLS = HALF // 16
BLOCKS = D // 32
GAIN = 2.5
FLOPS = 2 * NQ * N * D
BYTES = D * NQ * 4 + P * T * 4 + BLOCKS * T + T * 4 + P * (N // 16) * 2 + NQ * N * 4

BIAS_ROWS = (63, 127)
BIAS_CUT = 832
SCALE_STEP = P // BLOCKS
SCALE_CUT = 368
QUARTERS = N // P
TURN_RUNS = ((0, 2), (2, 1), (3, 1))
PIECES = ((0, 0), (0, 1), (0, 2), (0, 3), (1, 0), (1, 1), (1, 2), (1, 3))
SCORE_BANKS = ("turned2", "turned3", "turned0", "last", "spread0", "spread1", "spread2", "spread3")


def tile_attend_nrm_sig_topk_kernel(tc, qT, k_words, k_scales, kb, offs, out):
    nc = tc.nc
    with ExitStack() as ctx:
        sb = ctx.enter_context(tc.tile_pool(name="sb", bufs=1))
        shared = ctx.enter_context(tc.tile_pool(name="shared", bufs=1))
        ps = ctx.enter_context(tc.psum_pool(name="ps", bufs=1))

        offsets = sb.tile([P, N // 16], U16, name="offsets")
        kb_pool = sb.tile([P, T], F32, name="kb_pool", align_bytes=64)
        scale_pool = shared.tile([P, T // 4 + 1], I32, name="scale_pool", offset=0, align_bytes=64)
        word_pool = sb.tile([P, T], I32, name="word_pool", align_bytes=64)
        q_raw = sb.tile([P, 2, 2 * NQ], F32, name="q_raw", align_bytes=64)
        ident = sb.tile([P, P], F32, name="ident", align_bytes=64)
        key_scales = sb.tile([P, N // 4], I32, name="key_scales", align_bytes=64)

        q_pairs = qT[0].rearrange("(p a b) w -> p a (b w)", a=2, b=2)
        nc.sync.dma_start(q_raw[:, 0, 0 : 3 * P], q_pairs[:, 0, 0 : 3 * P])
        nc.sync.dma_start(offsets[:], offs)
        for row, tokens in zip(BIAS_ROWS, (slice(0, BIAS_CUT), slice(BIAS_CUT, T))):
            nc.scalar.dma_start(kb_pool[row : row + 1, tokens], kb[0:1, tokens])
        nc.vector.memset(scale_pool[:, SCALE_CUT:], 0)
        nc.gpsimd.memset(scale_pool[:, 0:SCALE_CUT], 0)
        nc.sync.dma_start(scale_pool[0:P:SCALE_STEP, 0 : T // 4], k_scales[0].bitcast(I32))
        nc.sync.dma_start(q_raw[:, 1, 0 : 3 * P], q_pairs[:, 1, 0 : 3 * P])
        nc.sync.dma_start(word_pool[:], k_words[0].rearrange("p t r -> p (t r)").bitcast(I32))
        nc.sync.dma_start(q_raw[:, :, 3 * P : 4 * P], q_pairs[:, :, 3 * P : 4 * P])

        make_identity(nc, ident[:])
        nc.gpsimd.memset(kb_pool[0 : BIAS_ROWS[1], BIAS_CUT:T], 0.0)
        nc.gpsimd.memset(key_scales[:], 0)
        zero = sb.tile([P, 1], F32, name="zero")
        nc.vector.memset(zero[:], 0.0)
        for rows in (slice(0, BIAS_ROWS[0]), slice(BIAS_ROWS[0] + 1, P)):
            nc.vector.memset(kb_pool[rows, 0 : BIAS_CUT - 1], 0.0)
            nc.vector.memset(kb_pool[rows, BIAS_CUT - 1 : BIAS_CUT], 0.0)

        unread = sb.tile([P, 1], F32, name="unread")
        nc.scalar.activation(unread[:], zero[:], ACT.Sigmoid)

        listed_scales = sb.tile([P, N], U8, name="listed_scales", align_bytes=64)
        nc.vector.tensor_copy(listed_scales[:], scale_pool[:, 0 : T // 4].bitcast(U8).indirect(offsets[:]))
        moves = []
        for quad in range(4):
            rows = slice(32 * quad, 32 * quad + 32, SCALE_STEP)
            moves.append((key_scales[32 * quad : 32 * quad + 4, :], listed_scales[rows, :].bitcast(I32)))
        for move in moves[:2]:
            nc.sync.dma_start(*move)

        def cast(g, copy):
            q_bf = shared.tile([P, P, PACK], BF16, name="q_bf%d" % g, offset=0, align_bytes=64)
            rows = q_raw[:].rearrange("p a (b g c i) -> p g c a b i", b=2, g=2, i=4)
            copy(q_bf[:].rearrange("p (c i) (a b) -> p c a b i", i=4, a=2), rows[:, g])
            return q_bf[:].rearrange("p w t -> p (w t)")

        first_bf = cast(0, nc.vector.tensor_copy)

        kb_listed = sb.tile([P, N - P], F32, name="kb_listed", tag="kb_listed", align_bytes=64)
        kb_last = shared.tile([P, P], F32, name="kb_last", offset=2 * P * PACK, align_bytes=64)
        listed = [kb_listed[:, s * P : (s + 1) * P] for s in range(QUARTERS - 1)] + [kb_last[:]]
        bias_col = sb.tile([P, QUARTERS], F32, name="bias_col", align_bytes=64)
        both = sb.tile([P, QUARTERS, 2], F32, name="both")
        bias = sb.tile([P, N], F32, name="bias", align_bytes=64)
        for first, last in ((0, 2), (2, 3)):
            part_list = offsets[:, P // 16 * first : P // 16 * last]
            nc.scalar.activation(kb_listed[:, first * P : last * P], kb_pool[:].indirect(part_list), ACT.Copy)
        for move in moves[2:]:
            nc.scalar.dma_start(*move)
        nc.scalar.activation(kb_last[:], kb_pool[:].indirect(offsets[:, P // 16 * (QUARTERS - 1) :]), ACT.Copy)
        for first, count in TURN_RUNS:
            turned = ps.tile([P, count, P], F32, name="turned%d" % first, tag="turned%d" % first)
            for u in range(count):
                s = first + u
                nc.tensor.transpose(turned[:, u, :], listed[s], ident[:])
            for u in range(count):
                s = first + u
                halves = turned[:, u, BIAS_ROWS[0] : P : P // 2]
                nc.scalar.activation(both[:, s, :], halves, ACT.Copy, accum_out=bias_col[:, s : s + 1])
        second_tile = sb.tile([P, P, PACK], BF16, name="second_tile", tag="kb_listed", align_bytes=64)
        by_row = q_raw[:].rearrange("p a (b g c i) -> p g b c a i", b=2, g=2, i=4)
        for b in range(2):
            nc.scalar.copy(second_tile[:].rearrange("p (c i) (a b) -> p b c a i", i=4, a=2)[:, b], by_row[:, 1, b])
        second_bf = second_tile[:].rearrange("p w t -> p (w t)")
        q_codes = [sb.tile([P, P], U32, name="q_codes%d" % g, align_bytes=64) for g in range(2)]
        q_scales = [sb.tile([P, P], U8, name="q_scales%d" % g, align_bytes=64) for g in range(2)]
        nc.vector.quantize_mx(q_codes[0][:].bitcast(FP8X4), q_scales[0][:], first_bf)

        for s in range(QUARTERS):
            spread = ps.tile([P, P], F32, name="spread%d" % s, tag="spread%d" % s)
            nc.tensor.transpose(spread[:], bias_col[:, s : s + 1].to_broadcast([P, P]), ident[:])
            nc.scalar.copy(bias[:, s * P : (s + 1) * P], spread[:])

        key_words = sb.tile([P, N], U32, name="key_words", align_bytes=64)
        for first, last in ((0, 1), (1, 2), (2, 3), (3, 4)):
            part_list = offsets[:, P // 16 * first : P // 16 * last]
            nc.vector.tensor_copy(key_words[:, first * P : last * P], word_pool[:].bitcast(U32).indirect(part_list))
        nc.vector.quantize_mx(q_codes[1][:].bitcast(FP8X4), q_scales[1][:], second_bf)
        logits = [sb.tile([P, N], F32, name="logits%d" % g, align_bytes=64) for g in range(2)]
        for i, (g, s) in enumerate(PIECES):
            piece = slice(s * P, (s + 1) * P)
            scores = ps.tile([P, P], F32, name="scores%d_%d" % (g, s), tag=SCORE_BANKS[i % len(SCORE_BANKS)])
            nc.tensor.matmul_mx(
                scores[:],
                lhsT=q_codes[g][:].bitcast(FP8X4),
                lhsT_scale=q_scales[g][:],
                rhs=key_words[:, piece].bitcast(FP8X4),
                rhs_scale=key_scales[:].bitcast(U8)[:, piece],
                start=True,
                stop=True,
            )
            nc.vector.tensor_tensor(logits[g][:, piece], scores[:], bias[:, piece], ALU.add)

        gates = [sb.tile([P, N], F32, name="gates%d" % g, align_bytes=64) for g in range(2)]
        total = [sb.tile([P, 1], F32, name="total%d" % g) for g in range(2)]
        inverse = [sb.tile([P, 1], F32, name="inverse%d" % g) for g in range(2)]
        result = [sb.tile([P, N], F32, name="result%d" % g, align_bytes=64) for g in range(2)]
        piece_sums = sb.tile([P, QUARTERS], F32, name="piece_sums")
        scaled_sums = sb.tile([P, QUARTERS], F32, name="scaled_sums")
        for s in range(QUARTERS):
            piece = slice(s * P, (s + 1) * P)
            nc.scalar.activation(gates[0][:, piece], logits[0][:, piece], ACT.Sigmoid, accum_out=piece_sums[:, s : s + 1])
        nc.scalar.activation(gates[1][:], logits[1][:], ACT.Sigmoid, accum_out=total[1][:])

        nc.vector.tensor_scalar(scaled_sums[:], piece_sums[:], 1.0 / GAIN, None, ALU.mult, ALU.add, accum_out=total[0][:])
        nc.vector.reciprocal(inverse[0][:], total[0][:])
        nc.vector.tensor_scalar(result[0][:, :HALF], gates[0][:, :HALF], inverse[0][:], None, ALU.mult)
        nc.sync.dma_start(out[0, 0:P, :HALF], result[0][:, :HALF])
        nc.scalar.activation(result[0][:, HALF:], gates[0][:, HALF:], ACT.Copy, scale=inverse[0][:])
        nc.sync.dma_start(out[0, 0:P, HALF:], result[0][:, HALF:])
        nc.vector.reciprocal(inverse[1][:], total[1][:])
        nc.vector.tensor_scalar(result[1][:], gates[1][:], inverse[1][:], GAIN, ALU.mult, ALU.mult)
        nc.sync.dma_start(out[0, P : 2 * P, :], result[1][:])
